import numpy as np
import ml_dtypes


def mxq(x, axis, fmt="e4m3"):
    dtype, down = {"e4m3": (ml_dtypes.float8_e4m3fn, 7), "e5m2": (ml_dtypes.float8_e5m2, 14)}[fmt]
    v = np.moveaxis(np.asarray(x, np.float32).astype(ml_dtypes.bfloat16).astype(np.float64), axis, -1)
    blocks = v.reshape(v.shape[:-1] + (-1, 32))
    amax = np.abs(blocks).max(-1, keepdims=True)
    byte = np.maximum(np.where(amax > 0, np.frexp(amax)[1] - 1 + 127, 0) - down, 1)
    scale = np.exp2(byte - 127.0)
    codes = (blocks / scale).astype(np.float32).astype(dtype).astype(np.float64)
    return np.moveaxis((codes * scale).reshape(v.shape), -1, axis)


WIDE = False


def mx_kscale(k):
    if not WIDE:
        return np.ones(k)
    levels = np.array([10, -10, 5, -5, 0])
    if k % 512:
        return np.exp2(np.random.permutation(np.resize(levels, k // 32))).repeat(32)
    a = np.empty((k // 512, 16))
    for p in range(k // 512):
        a[p, :8] = np.random.permutation(np.resize(levels, 8))
        for g in range(8):
            far = levels[np.abs(levels - a[p, g]) >= 10]
            a[p, g + 8] = far[np.random.randint(len(far))]
    return np.exp2(a.ravel()).repeat(32)


def f64(x):
    return np.asarray(x).astype(np.float64)


def striped(idx):
    return np.tile(idx.reshape(-1, 16).T, (8, 1)).astype(np.uint16)


def unstriped(offs):
    return offs[:16].T.reshape(-1).astype(np.int64)


K, T, S, V, N = 512, 1024, 512, 512, 1024


def setup_inputs():
    n = np.random.standard_normal
    s = mx_kscale(K)[:, None]
    return {
        "xT": (n((K, T)) * s).astype(np.float32),
        "w": (n((K, N)) / np.sqrt(K) / s).astype(np.float32),
        "b": (0.3 * n((V, 1))).astype(np.float32),
        "offs": striped(np.random.permutation(T)[:S]),
        "pos1": striped(np.random.permutation(N)[:V]),
    }


def reference(xT, w, b, offs, pos1):
    y = mxq(f64(w)[:, unstriped(pos1)], 0, "e4m3").T @ mxq(f64(xT)[:, unstriped(offs)], 0, "e4m3")
    return y + f64(b)

@@ -1,0 +1,155 @@
+from contextlib import ExitStack
+
+import concourse.mybir as mybir
+from concourse.masks import make_identity
+
+F32 = mybir.dt.float32
+BF16 = mybir.dt.bfloat16
+U16 = mybir.dt.uint16
+U32 = mybir.dt.uint32
+U8 = mybir.dt.uint8
+FP8X4 = mybir.dt.float8_e4m3fn_x4
+COPY = mybir.ActivationFunctionType.Copy
+IDENTITY = mybir.ActivationFunctionType.Identity
+ADD = mybir.AluOpType.add
+
+P = 128
+PACK = 4
+K, T, S, V, N = 512, 1024, 512, 512, 1024
+CHUNK = 128
+CHUNKS = V // CHUNK
+FLOPS = 2 * K * S * V
+
+
+def tile_picked_cross_bias_l_kernel(tc, xT, w, b, offs, pos1, out):
+    nc = tc.nc
+    with ExitStack() as ctx:
+        lists = ctx.enter_context(tc.tile_pool(name="lists", bufs=1))
+        keep = ctx.enter_context(tc.tile_pool(name="keep", bufs=1))
+        psum = ctx.enter_context(tc.psum_pool(name="psum", bufs=1))
+
+        offs_t = lists.tile([P, S // 16], U16, name="offs_t")
+        pos1_t = lists.tile([P, V // 16], U16, name="pos1_t")
+
+        x_rows = xT.rearrange("(p t) n -> p t n", t=PACK)
+        w_rows = w.rearrange("(p t) n -> p t n", t=PACK)
+        x_raw = [keep.tile([P, T], F32, name=f"x_raw{t}") for t in range(PACK)]
+        w_raw = [keep.tile([P, N], F32, name=f"w_raw{t}") for t in range(PACK)]
+
+        def load(tile, rows, t):
+            nc.sync.dma_start(out=tile[t][:], in_=rows[:, t, :])
+
+        load(x_raw, x_rows, 2)
+        nc.sync.dma_start(out=offs_t[:], in_=offs)
+        load(x_raw, x_rows, 3)
+        load(x_raw, x_rows, 0)
+        nc.sync.dma_start(out=pos1_t[:], in_=pos1)
+        load(w_raw, w_rows, 0)
+        load(x_raw, x_rows, 1)
+        load(w_raw, w_rows, 1)
+        load(w_raw, w_rows, 2)
+        load(w_raw, w_rows, 3)
+
+        warm = keep.tile([P, 2], F32, name="warm")
+        nc.vector.memset(warm[:], 0.0)
+        nc.scalar.activation(warm[:, 1:2], warm[:, 0:1], COPY)
+
+        b_rows = keep.tile([P, P], F32, name="b_rows")
+        nc.vector.memset(b_rows[:], 0.0)
+        nc.scalar.dma_start(out=b_rows[0:CHUNKS, :], in_=b.rearrange("(c p) o -> c (p o)", p=P))
+        ident = keep.tile([P, P], F32, name="ident")
+        make_identity(nc, ident[:])
+        b_turned = psum.tile([P, P], F32, name="b_turned")
+        nc.tensor.transpose(b_turned[:], b_rows[:], ident[:])
+        bias = keep.tile([P, CHUNKS], F32, name="bias")
+
+        w_g = keep.tile([P, 2, V], F32, name="w_g")
+        x_q = keep.tile([P, S, PACK], BF16, name="x_q", align_bytes=64)
+        w_q = keep.tile([P, V, PACK], BF16, name="w_q", align_bytes=64)
+        x_codes = keep.tile([P, S], U32, name="x_codes", align_bytes=64)
+        x_scales = keep.tile([P, S], U8, name="x_scales", align_bytes=64)
+        w_codes = keep.tile([P, V], U32, name="w_codes", align_bytes=64)
+        w_scales = keep.tile([P, V], U8, name="w_scales", align_bytes=64)
+
+        def quantise(codes, scales, src, cols):
+            nc.vector.quantize_mx(
+                out=codes[:, cols].bitcast(FP8X4),
+                scales=scales[:, cols],
+                in_=src[:, cols, :].rearrange("p c t -> p (c t)"),
+            )
+
+        every = slice(0, S)
+
+        x_half = {t: keep.tile([P, T], BF16, name=f"x_half{t}") for t in (2, 3)}
+        w_half = {t: keep.tile([P, N], BF16, name=f"w_half{t}") for t in (0, 1)}
+
+        def scalar_gather(dst, half, offsets, t):
+            nc.scalar.activation(dst[:, :, t], half[t][:].indirect(offsets[:]), COPY)
+
+        def vector_gather(dst, raw, offsets, t):
+            nc.vector.tensor_copy(dst[:, :, t], raw[t][:].indirect(offsets[:]))
+
+        nc.vector.tensor_copy(x_half[2][:], x_raw[2][:])
+        scalar_gather(x_q, x_half, offs_t, 2)
+        nc.vector.tensor_copy(x_half[3][:], x_raw[3][:])
+        scalar_gather(x_q, x_half, offs_t, 3)
+        vector_gather(x_q, x_raw, offs_t, 0)
+        nc.vector.tensor_copy(w_half[0][:], w_raw[0][:])
+        scalar_gather(w_q, w_half, pos1_t, 0)
+        vector_gather(x_q, x_raw, offs_t, 1)
+        nc.scalar.copy(out=w_half[1][:], in_=w_raw[1][:])
+        scalar_gather(w_q, w_half, pos1_t, 1)
+        nc.scalar.copy(out=bias[:], in_=b_turned[:, 0:CHUNKS])
+        quantise(x_codes, x_scales, x_q, every)
+        nc.vector.tensor_copy(w_g[:, 0, :], w_raw[2][:].indirect(pos1_t[:]))
+
+        def multiply(c, j0, width):
+            acc = psum.tile([P, width], F32, name=f"acc{c}_{j0}")
+            rows, cols = slice(CHUNK * c, CHUNK * (c + 1)), slice(j0, j0 + width)
+            nc.tensor.matmul_mx(
+                out=acc[:],
+                lhsT=w_codes[:, rows].bitcast(FP8X4),
+                lhsT_scale=w_scales[:, rows],
+                rhs=x_codes[:, cols].bitcast(FP8X4),
+                rhs_scale=x_scales[:, cols],
+                start=True,
+                stop=True,
+            )
+            result = keep.tile([P, width], F32, name=f"result{c}_{j0}")
+            if (c, j0) in ((1, 0), (3, 0)):
+                nc.vector.tensor_scalar(result[:], acc[:], bias[:, c : c + 1], None, op0=ADD)
+            else:
+                nc.scalar.activation(result[:], acc[:], IDENTITY, bias=bias[:, c : c + 1])
+            nc.sync.dma_start(out=out[rows, cols], in_=result[:])
+
+        def gather_last(c):
+            nc.vector.tensor_copy(
+                w_g[:, 1, CHUNK * c : CHUNK * (c + 1)],
+                w_raw[3][:].indirect(pos1_t[:, CHUNK // 16 * c : CHUNK // 16 * (c + 1)]),
+            )
+
+        def interleave(c):
+            rows = slice(CHUNK * c, CHUNK * (c + 1))
+            copy = nc.vector.tensor_copy if c == 0 else nc.scalar.copy
+            copy(out=w_q[:, rows, 2:4], in_=w_g[:, :, rows].rearrange("p t c -> p c t"))
+
+        def quantise_words(c):
+            quantise(w_codes, w_scales, w_q, slice(CHUNK * c, CHUNK * (c + 1)))
+
+        gather_last(0)
+        gather_last(1)
+        interleave(0)
+        interleave(1)
+        gather_last(2)
+        interleave(2)
+        quantise_words(0)
+        gather_last(3)
+        interleave(3)
+        quantise_words(1)
+        quantise_words(2)
+        quantise_words(3)
+        multiply(0, 0, S)
+        multiply(1, 0, S)
+        multiply(2, 0, S)
+        multiply(3, 0, S // 2)
+        multiply(3, S // 2, S // 2)

@@ -5,6 +5,7 @@ from concourse.masks import make_identity
 
 F32 = mybir.dt.float32
 BF16 = mybir.dt.bfloat16
+I32 = mybir.dt.int32
 U16 = mybir.dt.uint16
 U32 = mybir.dt.uint32
 U8 = mybir.dt.uint8
@@ -14,10 +15,10 @@ IDENTITY = mybir.ActivationFunctionType.Identity
 ADD = mybir.AluOpType.add
 
 P = 128
-PACK = 4
 K, T, S, V, N = 512, 1024, 512, 512, 1024
 CHUNK = 128
 CHUNKS = V // CHUNK
+SPLIT = 576
 FLOPS = 2 * K * S * V
 
 
@@ -31,24 +32,23 @@ def tile_picked_cross_bias_l_kernel(tc, xT, w, b, offs, pos1, out):
         offs_t = lists.tile([P, S // 16], U16, name="offs_t")
         pos1_t = lists.tile([P, V // 16], U16, name="pos1_t")
 
-        x_rows = xT.rearrange("(p t) n -> p t n", t=PACK)
-        w_rows = w.rearrange("(p t) n -> p t n", t=PACK)
-        x_raw = [keep.tile([P, T], F32, name=f"x_raw{t}") for t in range(PACK)]
-        w_raw = [keep.tile([P, N], F32, name=f"w_raw{t}") for t in range(PACK)]
+        x_rows = xT.rearrange("(p u e) n -> p u e n", u=2, e=2)
+        w_rows = w.rearrange("(p u e) n -> p u e n", u=2, e=2)
 
-        def load(tile, rows, t):
-            nc.sync.dma_start(out=tile[t][:], in_=rows[:, t, :])
+        def load(rows, u, c0, c1, name):
+            raw = keep.tile([P, 2, c1 - c0], F32, name=name, tag=name)
+            nc.sync.dma_start(out=raw[:], in_=rows[:, u, :, c0:c1])
+            return raw
 
-        load(x_raw, x_rows, 2)
+        x0 = load(x_rows, 0, 0, T, "x0")
         nc.sync.dma_start(out=offs_t[:], in_=offs)
-        load(x_raw, x_rows, 3)
-        load(x_raw, x_rows, 0)
+        x1a = load(x_rows, 1, 0, SPLIT, "x1a")
+        x1b = load(x_rows, 1, SPLIT, T, "x1b")
         nc.sync.dma_start(out=pos1_t[:], in_=pos1)
-        load(w_raw, w_rows, 0)
-        load(x_raw, x_rows, 1)
-        load(w_raw, w_rows, 1)
-        load(w_raw, w_rows, 2)
-        load(w_raw, w_rows, 3)
+        w0a = load(w_rows, 0, 0, 512, "w0a")
+        w0b = load(w_rows, 0, 512, N, "w0b")
+        w1a = load(w_rows, 1, 0, SPLIT, "w1a")
+        w1b = load(w_rows, 1, SPLIT, N, "w1b")
 
         warm = keep.tile([P, 2], F32, name="warm")
         nc.vector.memset(warm[:], 0.0)
@@ -62,48 +62,91 @@ def tile_picked_cross_bias_l_kernel(tc, xT, w, b, offs, pos1, out):
         b_turned = psum.tile([P, P], F32, name="b_turned")
         nc.tensor.transpose(b_turned[:], b_rows[:], ident[:])
         bias = keep.tile([P, CHUNKS], F32, name="bias")
+        nc.vector.tensor_copy(bias[:], b_turned[:, 0:CHUNKS])
 
-        w_g = keep.tile([P, 2, V], F32, name="w_g")
-        x_q = keep.tile([P, S, PACK], BF16, name="x_q", align_bytes=64)
-        w_q = keep.tile([P, V, PACK], BF16, name="w_q", align_bytes=64)
+        x_pairs = [keep.tile([P, 2 * T], BF16, name=f"x_pairs{u}") for u in range(2)]
+        w_pairs = [keep.tile([P, 2 * N], BF16, name=f"w_pairs{u}") for u in range(2)]
+        x_q = keep.tile([P, 4 * S], BF16, name="x_q", align_bytes=64)
         x_codes = keep.tile([P, S], U32, name="x_codes", align_bytes=64)
         x_scales = keep.tile([P, S], U8, name="x_scales", align_bytes=64)
         w_codes = keep.tile([P, V], U32, name="w_codes", align_bytes=64)
         w_scales = keep.tile([P, V], U8, name="w_scales", align_bytes=64)
 
-        def quantise(codes, scales, src, cols):
-            nc.vector.quantize_mx(
-                out=codes[:, cols].bitcast(FP8X4),
-                scales=scales[:, cols],
-                in_=src[:, cols, :].rearrange("p c t -> p (c t)"),
+        on_vector, on_scalar = nc.vector.tensor_copy, nc.scalar.copy
+
+        def cast(copy, pairs, raw, base, c0, c1):
+            copy(
+                out=pairs[:, 2 * (base + c0) : 2 * (base + c1)].rearrange("p (c e) -> p c e", e=2),
+                in_=raw[:, :, c0:c1].rearrange("p e c -> p c e"),
             )
 
-        every = slice(0, S)
+        def gather(dst, pairs, offsets, j0, j1):
+            nc.vector.tensor_copy(dst, pairs[:].bitcast(U32).indirect(offsets[:, j0 // 16 : j1 // 16]))
 
-        x_half = {t: keep.tile([P, T], BF16, name=f"x_half{t}") for t in (2, 3)}
-        w_half = {t: keep.tile([P, N], BF16, name=f"w_half{t}") for t in (0, 1)}
+        def planes(ap, dtype):
+            return ap.bitcast(dtype).rearrange("p (u c) -> p u c", u=2)
 
-        def scalar_gather(dst, half, offsets, t):
-            nc.scalar.activation(dst[:, :, t], half[t][:].indirect(offsets[:]), COPY)
+        def woven(ap, dtype):
+            return ap.bitcast(dtype).rearrange("p (c u) -> p c u", u=2)
 
-        def vector_gather(dst, raw, offsets, t):
-            nc.vector.tensor_copy(dst[:, :, t], raw[t][:].indirect(offsets[:]))
+        def weave(copy, dtype, dst, src):
+            copy(out=woven(dst, dtype), in_=src.bitcast(dtype).rearrange("p u c -> p c u"))
 
-        nc.vector.tensor_copy(x_half[2][:], x_raw[2][:])
-        scalar_gather(x_q, x_half, offs_t, 2)
-        nc.vector.tensor_copy(x_half[3][:], x_raw[3][:])
-        scalar_gather(x_q, x_half, offs_t, 3)
-        vector_gather(x_q, x_raw, offs_t, 0)
-        nc.vector.tensor_copy(w_half[0][:], w_raw[0][:])
-        scalar_gather(w_q, w_half, pos1_t, 0)
-        vector_gather(x_q, x_raw, offs_t, 1)
-        nc.scalar.copy(out=w_half[1][:], in_=w_raw[1][:])
-        scalar_gather(w_q, w_half, pos1_t, 1)
-        nc.scalar.copy(out=bias[:], in_=b_turned[:, 0:CHUNKS])
-        quantise(x_codes, x_scales, x_q, every)
-        nc.vector.tensor_copy(w_g[:, 0, :], w_raw[2][:].indirect(pos1_t[:]))
+        def quantise(codes, scales, j0, j1, src):
+            nc.vector.quantize_mx(out=codes[:, j0:j1].bitcast(FP8X4), scales=scales[:, j0:j1], in_=src)
 
-        def multiply(c, j0, width):
+        HEAD = 384
+        x_head = keep.tile([P, 4 * HEAD], BF16, name="x_head")
+        cast(on_scalar, x_pairs[0], x0, 0, 0, 336)
+        cast(on_vector, x_pairs[0], x0, 0, 336, 1024)
+        gather(planes(x_head[:], U32)[:, 0, :], x_pairs[0], offs_t, 0, HEAD)
+        cast(on_scalar, x_pairs[1], x1a, 0, 0, SPLIT)
+        cast(on_vector, x_pairs[1], x1b, SPLIT, 0, T - SPLIT)
+        x_rest = planes(keep.tile([P, 4 * (S - HEAD)], BF16, name="x_rest", tag="x1a")[:], U32)
+        gather(x_rest.bitcast(U32)[:, 0, :], x_pairs[0], offs_t, HEAD, S)
+        gather(planes(x_head[:], U32)[:, 1, :], x_pairs[1], offs_t, 0, HEAD)
+        gather(x_rest.bitcast(U32)[:, 1, :], x_pairs[1], offs_t, HEAD, S)
+        cast(on_scalar, w_pairs[0], w0a, 0, 0, 512)
+        weave(on_vector, I32, x_q[:, 0 : 4 * HEAD], planes(x_head[:], U32))
+        weave(on_vector, I32, x_q[:, 4 * HEAD : 4 * S], x_rest)
+        quantise(x_codes, x_scales, 0, S // 2, x_q[:, 0 : 2 * S])
+        cast(on_scalar, w_pairs[0], w0b, 512, 0, 512)
+        quantise(x_codes, x_scales, S // 2, S, x_q[:, 2 * S : 4 * S])
+
+        w_q = [keep.tile([P, 4 * CHUNK], BF16, name=f"w_q{c}", tag=f"w_q{c}", align_bytes=64)[:] for c in range(CHUNKS)]
+        third = keep.tile([P, 4 * CHUNK], BF16, name="third")
+
+        def gather_words(dst, c, u):
+            gather(dst[:, u, :], w_pairs[u], pos1_t, CHUNK * c, CHUNK * (c + 1))
+
+        def quantise_words(c):
+            quantise(w_codes, w_scales, CHUNK * c, CHUNK * (c + 1), w_q[c])
+
+        words = [
+            woven(w_q[0], U32).rearrange("p c u -> p u c"),
+            None,
+            planes(third[:], U32),
+        ]
+        gather_words(words[0], 0, 0)
+        gather_words(words[2], 2, 0)
+        cast(on_scalar, w_pairs[1], w1a, 0, 0, SPLIT)
+        cast(on_vector, w_pairs[1], w1b, SPLIT, 0, N - SPLIT)
+        words[1] = planes(keep.tile([P, 4 * CHUNK], BF16, name="second", tag="w1a")[:], U32)
+        gather_words(words[1], 1, 0)
+        gather_words(words[0], 0, 1)
+        gather_words(words[1], 1, 1)
+        weave(on_scalar, U32, w_q[1], words[1])
+        gather_words(words[2], 2, 1)
+        weave(on_scalar, U32, w_q[2], words[2])
+        quantise_words(0)
+        gather_words(words[1], 3, 0)
+        quantise_words(1)
+        gather_words(words[1], 3, 1)
+        quantise_words(2)
+        weave(on_vector, I32, w_q[3], words[1])
+        quantise_words(3)
+
+        def multiply(c, j0, width, engine, tag):
             acc = psum.tile([P, width], F32, name=f"acc{c}_{j0}")
             rows, cols = slice(CHUNK * c, CHUNK * (c + 1)), slice(j0, j0 + width)
             nc.tensor.matmul_mx(
@@ -115,41 +158,16 @@ def tile_picked_cross_bias_l_kernel(tc, xT, w, b, offs, pos1, out):
                 start=True,
                 stop=True,
             )
-            result = keep.tile([P, width], F32, name=f"result{c}_{j0}")
-            if (c, j0) in ((1, 0), (3, 0)):
+            result = keep.tile([P, width], F32, name=f"result{c}_{j0}", tag=tag, align_bytes=64)
+            if engine == "vector":
                 nc.vector.tensor_scalar(result[:], acc[:], bias[:, c : c + 1], None, op0=ADD)
             else:
                 nc.scalar.activation(result[:], acc[:], IDENTITY, bias=bias[:, c : c + 1])
             nc.sync.dma_start(out=out[rows, cols], in_=result[:])
 
-        def gather_last(c):
-            nc.vector.tensor_copy(
-                w_g[:, 1, CHUNK * c : CHUNK * (c + 1)],
-                w_raw[3][:].indirect(pos1_t[:, CHUNK // 16 * c : CHUNK // 16 * (c + 1)]),
-            )
-
-        def interleave(c):
-            rows = slice(CHUNK * c, CHUNK * (c + 1))
-            copy = nc.vector.tensor_copy if c == 0 else nc.scalar.copy
-            copy(out=w_q[:, rows, 2:4], in_=w_g[:, :, rows].rearrange("p t c -> p c t"))
-
-        def quantise_words(c):
-            quantise(w_codes, w_scales, w_q, slice(CHUNK * c, CHUNK * (c + 1)))
-
-        gather_last(0)
-        gather_last(1)
-        interleave(0)
-        interleave(1)
-        gather_last(2)
-        interleave(2)
-        quantise_words(0)
-        gather_last(3)
-        interleave(3)
-        quantise_words(1)
-        quantise_words(2)
-        quantise_words(3)
-        multiply(0, 0, S)
-        multiply(1, 0, S)
-        multiply(2, 0, S)
-        multiply(3, 0, S // 2)
-        multiply(3, S // 2, S // 2)
+        multiply(0, 0, S // 2, "scalar", "r0")
+        multiply(0, S // 2, S // 2, "scalar", "r1")
+        multiply(1, 0, S, "scalar", "r2")
+        multiply(2, 0, S, "vector", "w_q3")
+        multiply(3, 0, S // 2, "scalar", "r3")
+        multiply(3, S // 2, S // 2, "vector", "r4")

@@ -18,7 +18,7 @@ P = 128
 K, T, S, V, N = 512, 1024, 512, 512, 1024
 CHUNK = 128
 CHUNKS = V // CHUNK
-SPLIT = 576
+HALF = 512
 FLOPS = 2 * K * S * V
 
 
@@ -35,20 +35,21 @@ def tile_picked_cross_bias_l_kernel(tc, xT, w, b, offs, pos1, out):
         x_rows = xT.rearrange("(p u e) n -> p u e n", u=2, e=2)
         w_rows = w.rearrange("(p u e) n -> p u e n", u=2, e=2)
 
-        def load(rows, u, c0, c1, name):
-            raw = keep.tile([P, 2, c1 - c0], F32, name=name, tag=name)
+        def load(rows, u, name, c0=0, c1=T):
+            raw = keep.tile([P, 2, c1 - c0], F32, name=name, tag=name, align_bytes=64)
             nc.sync.dma_start(out=raw[:], in_=rows[:, u, :, c0:c1])
             return raw
 
-        x0 = load(x_rows, 0, 0, T, "x0")
+        x0a = load(x_rows, 0, "x0a", 0, HALF)
+        x0b = load(x_rows, 0, "x0b", HALF, T)
         nc.sync.dma_start(out=offs_t[:], in_=offs)
-        x1a = load(x_rows, 1, 0, SPLIT, "x1a")
-        x1b = load(x_rows, 1, SPLIT, T, "x1b")
+        x1a = load(x_rows, 1, "x1a", 0, HALF)
+        x1b = load(x_rows, 1, "x1b", HALF, T)
+        w0a = load(w_rows, 0, "w0a", 0, HALF)
+        w0b = load(w_rows, 0, "w0b", HALF, N)
         nc.sync.dma_start(out=pos1_t[:], in_=pos1)
-        w0a = load(w_rows, 0, 0, 512, "w0a")
-        w0b = load(w_rows, 0, 512, N, "w0b")
-        w1a = load(w_rows, 1, 0, SPLIT, "w1a")
-        w1b = load(w_rows, 1, SPLIT, N, "w1b")
+        w1a = load(w_rows, 1, "w1a", 0, HALF)
+        w1b = load(w_rows, 1, "w1b", HALF, N)
 
         warm = keep.tile([P, 2], F32, name="warm")
         nc.vector.memset(warm[:], 0.0)
@@ -59,10 +60,10 @@ def tile_picked_cross_bias_l_kernel(tc, xT, w, b, offs, pos1, out):
         nc.scalar.dma_start(out=b_rows[0:CHUNKS, :], in_=b.rearrange("(c p) o -> c (p o)", p=P))
         ident = keep.tile([P, P], F32, name="ident")
         make_identity(nc, ident[:])
-        b_turned = psum.tile([P, P], F32, name="b_turned")
+        b_turned = psum.tile([P, P], F32, name="b_turned", tag="bank0")
         nc.tensor.transpose(b_turned[:], b_rows[:], ident[:])
         bias = keep.tile([P, CHUNKS], F32, name="bias")
-        nc.vector.tensor_copy(bias[:], b_turned[:, 0:CHUNKS])
+        nc.scalar.copy(out=bias[:], in_=b_turned[:, 0:CHUNKS])
 
         x_pairs = [keep.tile([P, 2 * T], BF16, name=f"x_pairs{u}") for u in range(2)]
         w_pairs = [keep.tile([P, 2 * N], BF16, name=f"w_pairs{u}") for u in range(2)]
@@ -95,26 +96,25 @@ def tile_picked_cross_bias_l_kernel(tc, xT, w, b, offs, pos1, out):
         def quantise(codes, scales, j0, j1, src):
             nc.vector.quantize_mx(out=codes[:, j0:j1].bitcast(FP8X4), scales=scales[:, j0:j1], in_=src)
 
-        HEAD = 384
-        x_head = keep.tile([P, 4 * HEAD], BF16, name="x_head")
-        cast(on_scalar, x_pairs[0], x0, 0, 0, 336)
-        cast(on_vector, x_pairs[0], x0, 0, 336, 1024)
-        gather(planes(x_head[:], U32)[:, 0, :], x_pairs[0], offs_t, 0, HEAD)
-        cast(on_scalar, x_pairs[1], x1a, 0, 0, SPLIT)
-        cast(on_vector, x_pairs[1], x1b, SPLIT, 0, T - SPLIT)
-        x_rest = planes(keep.tile([P, 4 * (S - HEAD)], BF16, name="x_rest", tag="x1a")[:], U32)
-        gather(x_rest.bitcast(U32)[:, 0, :], x_pairs[0], offs_t, HEAD, S)
-        gather(planes(x_head[:], U32)[:, 1, :], x_pairs[1], offs_t, 0, HEAD)
-        gather(x_rest.bitcast(U32)[:, 1, :], x_pairs[1], offs_t, HEAD, S)
-        cast(on_scalar, w_pairs[0], w0a, 0, 0, 512)
-        weave(on_vector, I32, x_q[:, 0 : 4 * HEAD], planes(x_head[:], U32))
-        weave(on_vector, I32, x_q[:, 4 * HEAD : 4 * S], x_rest)
-        quantise(x_codes, x_scales, 0, S // 2, x_q[:, 0 : 2 * S])
-        cast(on_scalar, w_pairs[0], w0b, 512, 0, 512)
-        quantise(x_codes, x_scales, S // 2, S, x_q[:, 2 * S : 4 * S])
+        x_words = planes(keep.tile([P, 4 * S], BF16, name="x_words")[:], U32)
+        cast(on_scalar, x_pairs[0], x0a, 0, 0, HALF)
+        cast(on_scalar, x_pairs[0], x0b, HALF, 0, 144)
+        cast(on_vector, x_pairs[0], x0b, HALF, 144, HALF)
+        gather(x_words[:, 0, :], x_pairs[0], offs_t, 0, S)
+        cast(on_scalar, x_pairs[1], x1a, 0, 0, HALF)
+        cast(on_scalar, x_pairs[1], x1b, HALF, 0, 128)
+        cast(on_vector, x_pairs[1], x1b, HALF, 128, HALF)
+        halves = [(0, S // 2), (S // 2, S)]
+        for j0, j1 in halves:
+            gather(x_words[:, 1, j0:j1], x_pairs[1], offs_t, j0, j1)
+        cast(on_scalar, w_pairs[0], w0a, 0, 0, HALF)
+        for j0, j1 in halves:
+            weave(on_vector, I32, x_q[:, 4 * j0 : 4 * j1], x_words[:, :, j0:j1])
+        cast(on_scalar, w_pairs[0], w0b, HALF, 0, HALF)
+        for j0, j1 in halves:
+            quantise(x_codes, x_scales, j0, j1, x_q[:, 4 * j0 : 4 * j1])
 
-        w_q = [keep.tile([P, 4 * CHUNK], BF16, name=f"w_q{c}", tag=f"w_q{c}", align_bytes=64)[:] for c in range(CHUNKS)]
-        third = keep.tile([P, 4 * CHUNK], BF16, name="third")
+        w_q = [keep.tile([P, 4 * CHUNK], BF16, name=f"w_q{c}", tag=f"w_q{c}", align_bytes=64)[:] for c in range(3)]
 
         def gather_words(dst, c, u):
             gather(dst[:, u, :], w_pairs[u], pos1_t, CHUNK * c, CHUNK * (c + 1))
@@ -122,52 +122,53 @@ def tile_picked_cross_bias_l_kernel(tc, xT, w, b, offs, pos1, out):
         def quantise_words(c):
             quantise(w_codes, w_scales, CHUNK * c, CHUNK * (c + 1), w_q[c])
 
-        words = [
-            woven(w_q[0], U32).rearrange("p c u -> p u c"),
-            None,
-            planes(third[:], U32),
-        ]
-        gather_words(words[0], 0, 0)
-        gather_words(words[2], 2, 0)
-        cast(on_scalar, w_pairs[1], w1a, 0, 0, SPLIT)
-        cast(on_vector, w_pairs[1], w1b, SPLIT, 0, N - SPLIT)
-        words[1] = planes(keep.tile([P, 4 * CHUNK], BF16, name="second", tag="w1a")[:], U32)
-        gather_words(words[1], 1, 0)
-        gather_words(words[0], 0, 1)
-        gather_words(words[1], 1, 1)
-        weave(on_scalar, U32, w_q[1], words[1])
-        gather_words(words[2], 2, 1)
-        weave(on_scalar, U32, w_q[2], words[2])
+        first = woven(w_q[0], U32).rearrange("p c u -> p u c")
+        third = planes(keep.tile([P, 4 * CHUNK], BF16, name="third")[:], U32)
+        cast(on_vector, w_pairs[1], w1a, 0, 256, HALF)
+        gather_words(first, 0, 0)
+        gather_words(third, 2, 0)
+        cast(on_scalar, w_pairs[1], w1a, 0, 0, 256)
+        cast(on_scalar, w_pairs[1], w1b, HALF, 0, 64)
+        cast(on_scalar, w_pairs[1], w1b, HALF, 64, 208)
+        cast(on_vector, w_pairs[1], w1b, HALF, 208, HALF)
+        second = w1b[:, :, 0:CHUNK].bitcast(U32).rearrange("p r (u i) -> p u r i", u=2)
+        gather(second[:, 0, :, :], w_pairs[0], pos1_t, CHUNK, 2 * CHUNK)
+        gather(second[:, 1, :, :], w_pairs[1], pos1_t, CHUNK, 2 * CHUNK)
+        on_scalar(
+            out=w_q[1].bitcast(U32).rearrange("p (r i u) -> p r i u", r=2, u=2),
+            in_=second.rearrange("p u r i -> p r i u"),
+        )
+        gather_words(first, 0, 1)
+        gather_words(third, 2, 1)
+        weave(on_scalar, U32, w_q[2], third)
         quantise_words(0)
-        gather_words(words[1], 3, 0)
         quantise_words(1)
-        gather_words(words[1], 3, 1)
+        w_q.append(w1b[:, 0, :].bitcast(BF16)[:, 0 : 4 * CHUNK])
+        fourth = woven(w_q[3], U32).rearrange("p c u -> p u c")
+        gather_words(fourth, 3, 0)
+        gather_words(fourth, 3, 1)
         quantise_words(2)
-        weave(on_vector, I32, w_q[3], words[1])
         quantise_words(3)
 
-        def multiply(c, j0, width, engine, tag):
-            acc = psum.tile([P, width], F32, name=f"acc{c}_{j0}")
-            rows, cols = slice(CHUNK * c, CHUNK * (c + 1)), slice(j0, j0 + width)
-            nc.tensor.matmul_mx(
-                out=acc[:],
-                lhsT=w_codes[:, rows].bitcast(FP8X4),
-                lhsT_scale=w_scales[:, rows],
-                rhs=x_codes[:, cols].bitcast(FP8X4),
-                rhs_scale=x_scales[:, cols],
-                start=True,
-                stop=True,
-            )
-            result = keep.tile([P, width], F32, name=f"result{c}_{j0}", tag=tag, align_bytes=64)
-            if engine == "vector":
-                nc.vector.tensor_scalar(result[:], acc[:], bias[:, c : c + 1], None, op0=ADD)
-            else:
-                nc.scalar.activation(result[:], acc[:], IDENTITY, bias=bias[:, c : c + 1])
-            nc.sync.dma_start(out=out[rows, cols], in_=result[:])
-
-        multiply(0, 0, S // 2, "scalar", "r0")
-        multiply(0, S // 2, S // 2, "scalar", "r1")
-        multiply(1, 0, S, "scalar", "r2")
-        multiply(2, 0, S, "vector", "w_q3")
-        multiply(3, 0, S // 2, "scalar", "r3")
-        multiply(3, S // 2, S // 2, "vector", "r4")
+        from_vector = keep.tile([P, CHUNKS - 1, S // 2], F32, name="from_vector", tag="w1b", align_bytes=64)
+        from_scalar = keep.tile([P, CHUNKS + 1, S // 2], F32, name="from_scalar")
+        for c in range(CHUNKS):
+            rows = slice(CHUNK * c, CHUNK * (c + 1))
+            for h, (j0, j1) in enumerate(halves):
+                acc = psum.tile([P, S // 2], F32, name=f"acc{c}_{h}", tag=f"bank{(2 * c + h + 1) % 8}")
+                nc.tensor.matmul_mx(
+                    out=acc[:],
+                    lhsT=w_codes[:, rows].bitcast(FP8X4),
+                    lhsT_scale=w_scales[:, rows],
+                    rhs=x_codes[:, j0:j1].bitcast(FP8X4),
+                    rhs_scale=x_scales[:, j0:j1],
+                    start=True,
+                    stop=True,
+                )
+                if c > 0 and h == 1:
+                    result = from_vector[:, c - 1, :]
+                    nc.vector.tensor_scalar(result, acc[:], bias[:, c : c + 1], None, op0=ADD)
+                else:
+                    result = from_scalar[:, CHUNKS if h == 1 else c, :]
+                    nc.scalar.activation(result, acc[:], IDENTITY, bias=bias[:, c : c + 1])
+                nc.sync.dma_start(out=out[rows, j0:j1], in_=result)

@@ -19,6 +19,7 @@ K, T, S, V, N = 512, 1024, 512, 512, 1024
 CHUNK = 128
 CHUNKS = V // CHUNK
 HALF = 512
+SPLIT = 512
 FLOPS = 2 * K * S * V
 
 
@@ -40,26 +41,20 @@ def tile_picked_cross_bias_l_kernel(tc, xT, w, b, offs, pos1, out):
             nc.sync.dma_start(out=raw[:], in_=rows[:, u, :, c0:c1])
             return raw
 
-        x0a = load(x_rows, 0, "x0a", 0, HALF)
-        x0b = load(x_rows, 0, "x0b", HALF, T)
+        x0 = load(x_rows, 0, "x0")
         nc.sync.dma_start(out=offs_t[:], in_=offs)
-        x1a = load(x_rows, 1, "x1a", 0, HALF)
-        x1b = load(x_rows, 1, "x1b", HALF, T)
+        x1 = load(x_rows, 1, "x1")
         w0a = load(w_rows, 0, "w0a", 0, HALF)
         w0b = load(w_rows, 0, "w0b", HALF, N)
         nc.sync.dma_start(out=pos1_t[:], in_=pos1)
-        w1a = load(w_rows, 1, "w1a", 0, HALF)
-        w1b = load(w_rows, 1, "w1b", HALF, N)
+        w1a = load(w_rows, 1, "w1a", 0, SPLIT)
+        w1b = load(w_rows, 1, "w1b", SPLIT, N)
 
-        warm = keep.tile([P, 2], F32, name="warm")
-        nc.vector.memset(warm[:], 0.0)
-        nc.scalar.activation(warm[:, 1:2], warm[:, 0:1], COPY)
-
-        b_rows = keep.tile([P, P], F32, name="b_rows")
-        nc.vector.memset(b_rows[:], 0.0)
-        nc.scalar.dma_start(out=b_rows[0:CHUNKS, :], in_=b.rearrange("(c p) o -> c (p o)", p=P))
         ident = keep.tile([P, P], F32, name="ident")
         make_identity(nc, ident[:])
+        b_rows = keep.tile([P, P], F32, name="b_rows")
+        nc.scalar.activation(b_rows[:], ident[:], COPY, scale=0.0)
+        nc.sync.dma_start(out=b_rows[0:CHUNKS, :], in_=b.rearrange("(c p) o -> c (p o)", p=P))
         b_turned = psum.tile([P, P], F32, name="b_turned", tag="bank0")
         nc.tensor.transpose(b_turned[:], b_rows[:], ident[:])
         bias = keep.tile([P, CHUNKS], F32, name="bias")
@@ -77,8 +72,8 @@ def tile_picked_cross_bias_l_kernel(tc, xT, w, b, offs, pos1, out):
 
         def cast(copy, pairs, raw, base, c0, c1):
             copy(
-                out=pairs[:, 2 * (base + c0) : 2 * (base + c1)].rearrange("p (c e) -> p c e", e=2),
-                in_=raw[:, :, c0:c1].rearrange("p e c -> p c e"),
+                out=pairs[:, 2 * (base + c0) : 2 * (base + c1)].rearrange("p (c i e) -> p c e i", i=4, e=2),
+                in_=raw[:, :, c0:c1].rearrange("p e (c i) -> p c e i", i=4),
             )
 
         def gather(dst, pairs, offsets, j0, j1):
@@ -91,19 +86,20 @@ def tile_picked_cross_bias_l_kernel(tc, xT, w, b, offs, pos1, out):
             return ap.bitcast(dtype).rearrange("p (c u) -> p c u", u=2)
 
         def weave(copy, dtype, dst, src):
-            copy(out=woven(dst, dtype), in_=src.bitcast(dtype).rearrange("p u c -> p c u"))
+            copy(
+                out=dst.bitcast(dtype).rearrange("p (c i u) -> p c u i", i=2, u=2),
+                in_=src.bitcast(dtype).rearrange("p u (c i) -> p c u i", i=2),
+            )
 
         def quantise(codes, scales, j0, j1, src):
             nc.vector.quantize_mx(out=codes[:, j0:j1].bitcast(FP8X4), scales=scales[:, j0:j1], in_=src)
 
         x_words = planes(keep.tile([P, 4 * S], BF16, name="x_words")[:], U32)
-        cast(on_scalar, x_pairs[0], x0a, 0, 0, HALF)
-        cast(on_scalar, x_pairs[0], x0b, HALF, 0, 144)
-        cast(on_vector, x_pairs[0], x0b, HALF, 144, HALF)
+        cast(on_scalar, x_pairs[0], x0, 0, 0, 336)
+        cast(on_vector, x_pairs[0], x0, 0, 336, T)
         gather(x_words[:, 0, :], x_pairs[0], offs_t, 0, S)
-        cast(on_scalar, x_pairs[1], x1a, 0, 0, HALF)
-        cast(on_scalar, x_pairs[1], x1b, HALF, 0, 128)
-        cast(on_vector, x_pairs[1], x1b, HALF, 128, HALF)
+        cast(on_scalar, x_pairs[1], x1, 0, 0, 336)
+        cast(on_vector, x_pairs[1], x1, 0, 336, T)
         halves = [(0, S // 2), (S // 2, S)]
         for j0, j1 in halves:
             gather(x_words[:, 1, j0:j1], x_pairs[1], offs_t, j0, j1)
@@ -114,7 +110,7 @@ def tile_picked_cross_bias_l_kernel(tc, xT, w, b, offs, pos1, out):
         for j0, j1 in halves:
             quantise(x_codes, x_scales, j0, j1, x_q[:, 4 * j0 : 4 * j1])
 
-        w_q = [keep.tile([P, 4 * CHUNK], BF16, name=f"w_q{c}", tag=f"w_q{c}", align_bytes=64)[:] for c in range(3)]
+        w_q = [keep.tile([P, 4 * CHUNK], BF16, name=f"w_q{c}", tag=f"w_q{c}", align_bytes=64)[:] for c in range(CHUNKS)]
 
         def gather_words(dst, c, u):
             gather(dst[:, u, :], w_pairs[u], pos1_t, CHUNK * c, CHUNK * (c + 1))
@@ -124,36 +120,30 @@ def tile_picked_cross_bias_l_kernel(tc, xT, w, b, offs, pos1, out):
 
         first = woven(w_q[0], U32).rearrange("p c u -> p u c")
         third = planes(keep.tile([P, 4 * CHUNK], BF16, name="third")[:], U32)
-        cast(on_vector, w_pairs[1], w1a, 0, 256, HALF)
         gather_words(first, 0, 0)
         gather_words(third, 2, 0)
-        cast(on_scalar, w_pairs[1], w1a, 0, 0, 256)
-        cast(on_scalar, w_pairs[1], w1b, HALF, 0, 64)
-        cast(on_scalar, w_pairs[1], w1b, HALF, 64, 208)
-        cast(on_vector, w_pairs[1], w1b, HALF, 208, HALF)
-        second = w1b[:, :, 0:CHUNK].bitcast(U32).rearrange("p r (u i) -> p u r i", u=2)
-        gather(second[:, 0, :, :], w_pairs[0], pos1_t, CHUNK, 2 * CHUNK)
-        gather(second[:, 1, :, :], w_pairs[1], pos1_t, CHUNK, 2 * CHUNK)
-        on_scalar(
-            out=w_q[1].bitcast(U32).rearrange("p (r i u) -> p r i u", r=2, u=2),
-            in_=second.rearrange("p u r i -> p r i u"),
-        )
+        cast(on_scalar, w_pairs[1], w1a, 0, 0, SPLIT)
+        cast(on_scalar, w_pairs[1], w1b, SPLIT, 0, 160)
+        cast(on_vector, w_pairs[1], w1b, SPLIT, 160, N - SPLIT)
+        second = w1a[:, :, 0:CHUNK].bitcast(U32)
+        gather_words(second, 1, 0)
+        gather_words(second, 1, 1)
+        weave(on_scalar, U32, w_q[1], second)
         gather_words(first, 0, 1)
         gather_words(third, 2, 1)
         weave(on_scalar, U32, w_q[2], third)
         quantise_words(0)
         quantise_words(1)
-        w_q.append(w1b[:, 0, :].bitcast(BF16)[:, 0 : 4 * CHUNK])
-        fourth = woven(w_q[3], U32).rearrange("p c u -> p u c")
-        gather_words(fourth, 3, 0)
-        gather_words(fourth, 3, 1)
+        gather_words(second, 3, 0)
+        gather_words(second, 3, 1)
         quantise_words(2)
+        weave(on_vector, I32, w_q[3], second)
         quantise_words(3)
 
-        from_vector = keep.tile([P, CHUNKS - 1, S // 2], F32, name="from_vector", tag="w1b", align_bytes=64)
-        from_scalar = keep.tile([P, CHUNKS + 1, S // 2], F32, name="from_scalar")
         for c in range(CHUNKS):
             rows = slice(CHUNK * c, CHUNK * (c + 1))
+            tag = "w_q3" if c == 2 else f"result{c}"
+            whole = keep.tile([P, S], F32, name=f"result{c}", tag=tag, align_bytes=64)
             for h, (j0, j1) in enumerate(halves):
                 acc = psum.tile([P, S // 2], F32, name=f"acc{c}_{h}", tag=f"bank{(2 * c + h + 1) % 8}")
                 nc.tensor.matmul_mx(
@@ -165,10 +155,12 @@ def tile_picked_cross_bias_l_kernel(tc, xT, w, b, offs, pos1, out):
                     start=True,
                     stop=True,
                 )
-                if c > 0 and h == 1:
-                    result = from_vector[:, c - 1, :]
+                result = whole[:, j0:j1]
+                if c >= 2 and h == 1:
                     nc.vector.tensor_scalar(result, acc[:], bias[:, c : c + 1], None, op0=ADD)
                 else:
-                    result = from_scalar[:, CHUNKS if h == 1 else c, :]
                     nc.scalar.activation(result, acc[:], IDENTITY, bias=bias[:, c : c + 1])
-                nc.sync.dma_start(out=out[rows, j0:j1], in_=result)
+                if c == 0:
+                    nc.sync.dma_start(out=out[rows, j0:j1], in_=result)
+            if c > 0:
+                nc.sync.dma_start(out=out[rows, :], in_=whole[:])

@@ -140,12 +140,18 @@ def tile_picked_cross_bias_l_kernel(tc, xT, w, b, offs, pos1, out):
         weave(on_vector, I32, w_q[3], second)
         quantise_words(3)
 
+        pieces = [
+            [(0, 128, 1), (128, 256, 0), (256, 512, 2)],
+            [(0, 256, 3), (256, 512, 4)],
+            [(0, 256, 5), (256, 512, 6)],
+            [(0, 256, 7), (256, 384, 1), (384, 512, 0)],
+        ]
         for c in range(CHUNKS):
             rows = slice(CHUNK * c, CHUNK * (c + 1))
             tag = "w_q3" if c == 2 else f"result{c}"
             whole = keep.tile([P, S], F32, name=f"result{c}", tag=tag, align_bytes=64)
-            for h, (j0, j1) in enumerate(halves):
-                acc = psum.tile([P, S // 2], F32, name=f"acc{c}_{h}", tag=f"bank{(2 * c + h + 1) % 8}")
+            for j0, j1, bank in pieces[c]:
+                acc = psum.tile([P, j1 - j0], F32, name=f"acc{c}_{j0}", tag=f"bank{bank}")
                 nc.tensor.matmul_mx(
                     out=acc[:],
                     lhsT=w_codes[:, rows].bitcast(FP8X4),
@@ -156,11 +162,11 @@ def tile_picked_cross_bias_l_kernel(tc, xT, w, b, offs, pos1, out):
                     stop=True,
                 )
                 result = whole[:, j0:j1]
-                if c >= 2 and h == 1:
+                if c >= 2 and j1 == S:
                     nc.vector.tensor_scalar(result, acc[:], bias[:, c : c + 1], None, op0=ADD)
                 else:
                     nc.scalar.activation(result, acc[:], IDENTITY, bias=bias[:, c : c + 1])
-                if c == 0:
-                    nc.sync.dma_start(out=out[rows, j0:j1], in_=result)
-            if c > 0:
+                if c in (0, 3) and j1 % 256 == 0:
+                    nc.sync.dma_start(out=out[rows, j1 - 256 : j1], in_=whole[:, j1 - 256 : j1])
+            if c in (1, 2):
                 nc.sync.dma_start(out=out[rows, :], in_=whole[:])

@@ -144,7 +144,7 @@ def tile_picked_cross_bias_l_kernel(tc, xT, w, b, offs, pos1, out):
             [(0, 128, 1), (128, 256, 0), (256, 512, 2)],
             [(0, 256, 3), (256, 512, 4)],
             [(0, 256, 5), (256, 512, 6)],
-            [(0, 256, 7), (256, 384, 1), (384, 512, 0)],
+            [(0, 256, 7), (256, 512, 1)],
         ]
         for c in range(CHUNKS):
             rows = slice(CHUNK * c, CHUNK * (c + 1))
@@ -166,7 +166,7 @@ def tile_picked_cross_bias_l_kernel(tc, xT, w, b, offs, pos1, out):
                     nc.vector.tensor_scalar(result, acc[:], bias[:, c : c + 1], None, op0=ADD)
                 else:
                     nc.scalar.activation(result, acc[:], IDENTITY, bias=bias[:, c : c + 1])
-                if c in (0, 3) and j1 % 256 == 0:
+                if c in (0, 1) and j1 % 256 == 0:
                     nc.sync.dma_start(out=out[rows, j1 - 256 : j1], in_=whole[:, j1 - 256 : j1])
-            if c in (1, 2):
+            if c in (2, 3):
                 nc.sync.dma_start(out=out[rows, :], in_=whole[:])

@@ -44,10 +44,13 @@ def tile_picked_cross_bias_l_kernel(tc, xT, w, b, offs, pos1, out):
         x0 = load(x_rows, 0, "x0")
         nc.sync.dma_start(out=offs_t[:], in_=offs)
         x1 = load(x_rows, 1, "x1")
-        w0a = load(w_rows, 0, "w0a", 0, HALF)
-        w0b = load(w_rows, 0, "w0b", HALF, N)
+        stage = keep.tile([P, 448 + 2 * N], F32, name="stage", align_bytes=64)
+        w0 = stage[:, 448:].rearrange("p (e n) -> p e n", e=2)
+        nc.sync.dma_start(out=w0, in_=w_rows[:, 0, :, :])
         nc.sync.dma_start(out=pos1_t[:], in_=pos1)
-        w1a = load(w_rows, 1, "w1a", 0, SPLIT)
+        slots = keep.tile([P, CHUNK + 2 * SPLIT], F32, name="slots", align_bytes=64)
+        w1a = slots[:, CHUNK:].rearrange("p (e n) -> p e n", e=2)
+        nc.sync.dma_start(out=w1a, in_=w_rows[:, 1, :, 0:SPLIT])
         w1b = load(w_rows, 1, "w1b", SPLIT, N)
 
         ident = keep.tile([P, P], F32, name="ident")
@@ -62,8 +65,7 @@ def tile_picked_cross_bias_l_kernel(tc, xT, w, b, offs, pos1, out):
 
         x_pairs = [keep.tile([P, 2 * T], BF16, name=f"x_pairs{u}") for u in range(2)]
         w_pairs = [keep.tile([P, 2 * N], BF16, name=f"w_pairs{u}") for u in range(2)]
-        x_q = keep.tile([P, 4 * S], BF16, name="x_q", align_bytes=64)
-        x_codes = keep.tile([P, S], U32, name="x_codes", align_bytes=64)
+        x_q0 = stage[:, 0:S].bitcast(BF16)
         x_scales = keep.tile([P, S], U8, name="x_scales", align_bytes=64)
         w_codes = keep.tile([P, V], U32, name="w_codes", align_bytes=64)
         w_scales = keep.tile([P, V], U8, name="w_scales", align_bytes=64)
@@ -91,24 +93,23 @@ def tile_picked_cross_bias_l_kernel(tc, xT, w, b, offs, pos1, out):
                 in_=src.bitcast(dtype).rearrange("p u (c i) -> p c u i", i=2),
             )
 
-        def quantise(codes, scales, j0, j1, src):
-            nc.vector.quantize_mx(out=codes[:, j0:j1].bitcast(FP8X4), scales=scales[:, j0:j1], in_=src)
+        def quantise(codes, scales, src):
+            nc.vector.quantize_mx(out=codes.bitcast(FP8X4), scales=scales, in_=src)
 
         x_words = planes(keep.tile([P, 4 * S], BF16, name="x_words")[:], U32)
         cast(on_scalar, x_pairs[0], x0, 0, 0, 336)
         cast(on_vector, x_pairs[0], x0, 0, 336, T)
         gather(x_words[:, 0, :], x_pairs[0], offs_t, 0, S)
-        cast(on_scalar, x_pairs[1], x1, 0, 0, 336)
-        cast(on_vector, x_pairs[1], x1, 0, 336, T)
+        cast(on_scalar, x_pairs[1], x1, 0, 0, 400)
+        cast(on_vector, x_pairs[1], x1, 0, 400, T)
         halves = [(0, S // 2), (S // 2, S)]
         for j0, j1 in halves:
             gather(x_words[:, 1, j0:j1], x_pairs[1], offs_t, j0, j1)
-        cast(on_scalar, w_pairs[0], w0a, 0, 0, HALF)
-        for j0, j1 in halves:
-            weave(on_vector, I32, x_q[:, 4 * j0 : 4 * j1], x_words[:, :, j0:j1])
-        cast(on_scalar, w_pairs[0], w0b, HALF, 0, HALF)
-        for j0, j1 in halves:
-            quantise(x_codes, x_scales, j0, j1, x_q[:, 4 * j0 : 4 * j1])
+        cast(on_scalar, w_pairs[0], w0, 0, 0, 64)
+        cast(on_scalar, w_pairs[0], w0, 0, 64, 480)
+        cast(on_vector, w_pairs[0], w0, 0, 480, N)
+        weave(on_vector, I32, x_q0, x_words[:, :, 0 : S // 2])
+        x_codes = [keep.tile([P, S // 2], U32, name=f"x_codes{h}", align_bytes=64)[:] for h in range(2)]
 
         w_q = [keep.tile([P, 4 * CHUNK], BF16, name=f"w_q{c}", tag=f"w_q{c}", align_bytes=64)[:] for c in range(CHUNKS)]
 
@@ -116,17 +117,23 @@ def tile_picked_cross_bias_l_kernel(tc, xT, w, b, offs, pos1, out):
             gather(dst[:, u, :], w_pairs[u], pos1_t, CHUNK * c, CHUNK * (c + 1))
 
         def quantise_words(c):
-            quantise(w_codes, w_scales, CHUNK * c, CHUNK * (c + 1), w_q[c])
+            picked = slice(CHUNK * c, CHUNK * (c + 1))
+            quantise(w_codes[:, picked], w_scales[:, picked], w_q[c])
 
         first = woven(w_q[0], U32).rearrange("p c u -> p u c")
         third = planes(keep.tile([P, 4 * CHUNK], BF16, name="third")[:], U32)
         gather_words(first, 0, 0)
+        quantise(x_codes[0], x_scales[:, 0 : S // 2], x_q0)
         gather_words(third, 2, 0)
+        fourth = slots[:, 0 : 2 * CHUNK].bitcast(U32).rearrange("p (u c) -> p u c", u=2)
+        gather_words(fourth, 3, 0)
         cast(on_scalar, w_pairs[1], w1a, 0, 0, SPLIT)
-        cast(on_scalar, w_pairs[1], w1b, SPLIT, 0, 160)
-        cast(on_vector, w_pairs[1], w1b, SPLIT, 160, N - SPLIT)
+        cast(on_scalar, w_pairs[1], w1b, SPLIT, 0, 256)
+        cast(on_vector, w_pairs[1], w1b, SPLIT, 256, N - SPLIT)
         second = w1a[:, :, 0:CHUNK].bitcast(U32)
         gather_words(second, 1, 0)
+        x_q1 = keep.tile([P, 2 * S], BF16, name="x_q1", tag="w1b", align_bytes=64)
+        weave(on_scalar, U32, x_q1[:], x_words[:, :, S // 2 : S])
         gather_words(second, 1, 1)
         weave(on_scalar, U32, w_q[1], second)
         gather_words(first, 0, 1)
@@ -134,39 +141,36 @@ def tile_picked_cross_bias_l_kernel(tc, xT, w, b, offs, pos1, out):
         weave(on_scalar, U32, w_q[2], third)
         quantise_words(0)
         quantise_words(1)
-        gather_words(second, 3, 0)
-        gather_words(second, 3, 1)
+        quantise(x_codes[1], x_scales[:, S // 2 : S], x_q1[:])
+        gather_words(fourth, 3, 1)
         quantise_words(2)
-        weave(on_vector, I32, w_q[3], second)
+        weave(on_vector, I32, w_q[3], fourth)
         quantise_words(3)
 
-        pieces = [
-            [(0, 128, 1), (128, 256, 0), (256, 512, 2)],
-            [(0, 256, 3), (256, 512, 4)],
-            [(0, 256, 5), (256, 512, 6)],
-            [(0, 256, 7), (256, 512, 1)],
+        results = [
+            keep.tile([P, S], F32, name=f"result{c}", tag="w_q3" if c == 2 else f"result{c}", align_bytes=64)
+            for c in range(CHUNKS)
         ]
-        for c in range(CHUNKS):
+        pieces = [(0, 0, 128), (0, 128, 256), (1, 0, 256), (0, 256, 512), (1, 256, 512)]
+        pieces = pieces + [(c, j0, j1) for c in (2, 3) for j0, j1 in halves]
+        for n, (c, j0, j1) in enumerate(pieces):
             rows = slice(CHUNK * c, CHUNK * (c + 1))
-            tag = "w_q3" if c == 2 else f"result{c}"
-            whole = keep.tile([P, S], F32, name=f"result{c}", tag=tag, align_bytes=64)
-            for j0, j1, bank in pieces[c]:
-                acc = psum.tile([P, j1 - j0], F32, name=f"acc{c}_{j0}", tag=f"bank{bank}")
-                nc.tensor.matmul_mx(
-                    out=acc[:],
-                    lhsT=w_codes[:, rows].bitcast(FP8X4),
-                    lhsT_scale=w_scales[:, rows],
-                    rhs=x_codes[:, j0:j1].bitcast(FP8X4),
-                    rhs_scale=x_scales[:, j0:j1],
-                    start=True,
-                    stop=True,
-                )
-                result = whole[:, j0:j1]
-                if c >= 2 and j1 == S:
-                    nc.vector.tensor_scalar(result, acc[:], bias[:, c : c + 1], None, op0=ADD)
-                else:
-                    nc.scalar.activation(result, acc[:], IDENTITY, bias=bias[:, c : c + 1])
-                if c in (0, 1) and j1 % 256 == 0:
-                    nc.sync.dma_start(out=out[rows, j1 - 256 : j1], in_=whole[:, j1 - 256 : j1])
-            if c in (2, 3):
-                nc.sync.dma_start(out=out[rows, :], in_=whole[:])
+            acc = psum.tile([P, j1 - j0], F32, name=f"acc{n}", tag=f"bank{(n + 1) % 8}")
+            nc.tensor.matmul_mx(
+                out=acc[:],
+                lhsT=w_codes[:, rows].bitcast(FP8X4),
+                lhsT_scale=w_scales[:, rows],
+                rhs=x_codes[j0 // 256][:, j0 % 256 : j0 % 256 + j1 - j0].bitcast(FP8X4),
+                rhs_scale=x_scales[:, j0:j1],
+                start=True,
+                stop=True,
+            )
+            result = results[c][:, j0:j1]
+            if c >= 2 and j1 == S:
+                nc.vector.tensor_scalar(result, acc[:], bias[:, c : c + 1], None, op0=ADD)
+            else:
+                nc.scalar.activation(result, acc[:], IDENTITY, bias=bias[:, c : c + 1])
+            if c < 2 and j1 % 256 == 0:
+                nc.sync.dma_start(out=out[rows, j1 - 256 : j1], in_=results[c][:, j1 - 256 : j1])
+            if c >= 2 and j1 == S:
+                nc.sync.dma_start(out=out[rows, :], in_=results[c][:])

@@ -18,9 +18,18 @@ P = 128
 K, T, S, V, N = 512, 1024, 512, 512, 1024
 CHUNK = 128
 CHUNKS = V // CHUNK
-HALF = 512
-SPLIT = 512
+HALF = S // 2
+QUARTER = S // 4
+PIECE = N // 2
+BANKS = 8
 FLOPS = 2 * K * S * V
+
+X0_ON_SCALAR = 336
+X1_ON_SCALAR = 368
+W0_ON_SCALAR = 320
+W1_ON_SCALAR = 208
+W0_EARLY = 320
+SHARED = 64
 
 
 def tile_picked_cross_bias_l_kernel(tc, xT, w, b, offs, pos1, out):
@@ -36,22 +45,26 @@ def tile_picked_cross_bias_l_kernel(tc, xT, w, b, offs, pos1, out):
         x_rows = xT.rearrange("(p u e) n -> p u e n", u=2, e=2)
         w_rows = w.rearrange("(p u e) n -> p u e n", u=2, e=2)
 
-        def load(rows, u, name, c0=0, c1=T):
+        def load(rows, u, name, c0, c1):
             raw = keep.tile([P, 2, c1 - c0], F32, name=name, tag=name, align_bytes=64)
             nc.sync.dma_start(out=raw[:], in_=rows[:, u, :, c0:c1])
             return raw
 
-        x0 = load(x_rows, 0, "x0")
+        x0 = load(x_rows, 0, "x0", 0, T)
         nc.sync.dma_start(out=offs_t[:], in_=offs)
-        x1 = load(x_rows, 1, "x1")
-        stage = keep.tile([P, 448 + 2 * N], F32, name="stage", align_bytes=64)
-        w0 = stage[:, 448:].rearrange("p (e n) -> p e n", e=2)
-        nc.sync.dma_start(out=w0, in_=w_rows[:, 0, :, :])
+        x1 = load(x_rows, 1, "x1", 0, T)
+        front = S - SHARED
+        stage = keep.tile([P, front + 2 * N], F32, name="stage", align_bytes=64)
+        w0 = stage[:, front:].rearrange("p (e n) -> p e n", e=2)
+        w0_run = w.rearrange("(p u e) n -> p u (e n)", u=2, e=2)[:, 0, :]
+        cut = N + W0_EARLY
+        nc.sync.dma_start(out=stage[:, front : front + cut], in_=w0_run[:, 0:cut])
+        nc.sync.dma_start(out=stage[:, front + cut :], in_=w0_run[:, cut:])
         nc.sync.dma_start(out=pos1_t[:], in_=pos1)
-        slots = keep.tile([P, CHUNK + 2 * SPLIT], F32, name="slots", align_bytes=64)
+        slots = keep.tile([P, CHUNK + 2 * PIECE], F32, name="slots", align_bytes=64)
         w1a = slots[:, CHUNK:].rearrange("p (e n) -> p e n", e=2)
-        nc.sync.dma_start(out=w1a, in_=w_rows[:, 1, :, 0:SPLIT])
-        w1b = load(w_rows, 1, "w1b", SPLIT, N)
+        nc.sync.dma_start(out=w1a, in_=w_rows[:, 1, :, 0:PIECE])
+        w1b = load(w_rows, 1, "w1b", PIECE, N)
 
         ident = keep.tile([P, P], F32, name="ident")
         make_identity(nc, ident[:])
@@ -65,7 +78,7 @@ def tile_picked_cross_bias_l_kernel(tc, xT, w, b, offs, pos1, out):
 
         x_pairs = [keep.tile([P, 2 * T], BF16, name=f"x_pairs{u}") for u in range(2)]
         w_pairs = [keep.tile([P, 2 * N], BF16, name=f"w_pairs{u}") for u in range(2)]
-        x_q0 = stage[:, 0:S].bitcast(BF16)
+        x_woven0 = stage[:, 0:S].bitcast(BF16)
         x_scales = keep.tile([P, S], U8, name="x_scales", align_bytes=64)
         w_codes = keep.tile([P, V], U32, name="w_codes", align_bytes=64)
         w_scales = keep.tile([P, V], U8, name="w_scales", align_bytes=64)
@@ -81,11 +94,8 @@ def tile_picked_cross_bias_l_kernel(tc, xT, w, b, offs, pos1, out):
         def gather(dst, pairs, offsets, j0, j1):
             nc.vector.tensor_copy(dst, pairs[:].bitcast(U32).indirect(offsets[:, j0 // 16 : j1 // 16]))
 
-        def planes(ap, dtype):
-            return ap.bitcast(dtype).rearrange("p (u c) -> p u c", u=2)
-
-        def woven(ap, dtype):
-            return ap.bitcast(dtype).rearrange("p (c u) -> p c u", u=2)
+        def by_pair(ap):
+            return ap.bitcast(U32).rearrange("p (u c) -> p u c", u=2)
 
         def weave(copy, dtype, dst, src):
             copy(
@@ -96,81 +106,87 @@ def tile_picked_cross_bias_l_kernel(tc, xT, w, b, offs, pos1, out):
         def quantise(codes, scales, src):
             nc.vector.quantize_mx(out=codes.bitcast(FP8X4), scales=scales, in_=src)
 
-        x_words = planes(keep.tile([P, 4 * S], BF16, name="x_words")[:], U32)
-        cast(on_scalar, x_pairs[0], x0, 0, 0, 336)
-        cast(on_vector, x_pairs[0], x0, 0, 336, T)
+        x_words = by_pair(keep.tile([P, 4 * S], BF16, name="x_words")[:])
+        cast(on_scalar, x_pairs[0], x0, 0, 0, X0_ON_SCALAR)
+        cast(on_vector, x_pairs[0], x0, 0, X0_ON_SCALAR, T)
         gather(x_words[:, 0, :], x_pairs[0], offs_t, 0, S)
-        cast(on_scalar, x_pairs[1], x1, 0, 0, 400)
-        cast(on_vector, x_pairs[1], x1, 0, 400, T)
-        halves = [(0, S // 2), (S // 2, S)]
+        cast(on_scalar, x_pairs[1], x1, 0, 0, X1_ON_SCALAR)
+        cast(on_vector, x_pairs[1], x1, 0, X1_ON_SCALAR, T)
+        halves = [(0, HALF), (HALF, S)]
         for j0, j1 in halves:
             gather(x_words[:, 1, j0:j1], x_pairs[1], offs_t, j0, j1)
-        cast(on_scalar, w_pairs[0], w0, 0, 0, 64)
-        cast(on_scalar, w_pairs[0], w0, 0, 64, 480)
-        cast(on_vector, w_pairs[0], w0, 0, 480, N)
-        weave(on_vector, I32, x_q0, x_words[:, :, 0 : S // 2])
-        x_codes = [keep.tile([P, S // 2], U32, name=f"x_codes{h}", align_bytes=64)[:] for h in range(2)]
 
-        w_q = [keep.tile([P, 4 * CHUNK], BF16, name=f"w_q{c}", tag=f"w_q{c}", align_bytes=64)[:] for c in range(CHUNKS)]
+        cast(on_scalar, w_pairs[0], w0, 0, 0, W0_EARLY)
+        cast(on_scalar, w_pairs[0], w0, 0, W0_EARLY, W0_EARLY + W0_ON_SCALAR)
+        cast(on_vector, w_pairs[0], w0, 0, W0_EARLY + W0_ON_SCALAR, N)
+        weave(on_vector, I32, x_woven0, x_words[:, :, 0:HALF])
+        x_codes = [keep.tile([P, HALF], U32, name=f"x_codes{h}", align_bytes=64)[:] for h in range(2)]
+
+        w_woven = [
+            keep.tile([P, 4 * CHUNK], BF16, name=f"w_woven{c}", tag=f"w_woven{c}", align_bytes=64)[:]
+            for c in range(CHUNKS)
+        ]
 
         def gather_words(dst, c, u):
             gather(dst[:, u, :], w_pairs[u], pos1_t, CHUNK * c, CHUNK * (c + 1))
 
         def quantise_words(c):
             picked = slice(CHUNK * c, CHUNK * (c + 1))
-            quantise(w_codes[:, picked], w_scales[:, picked], w_q[c])
+            quantise(w_codes[:, picked], w_scales[:, picked], w_woven[c])
 
-        first = woven(w_q[0], U32).rearrange("p c u -> p u c")
-        third = planes(keep.tile([P, 4 * CHUNK], BF16, name="third")[:], U32)
-        gather_words(first, 0, 0)
-        quantise(x_codes[0], x_scales[:, 0 : S // 2], x_q0)
-        gather_words(third, 2, 0)
-        fourth = slots[:, 0 : 2 * CHUNK].bitcast(U32).rearrange("p (u c) -> p u c", u=2)
-        gather_words(fourth, 3, 0)
-        cast(on_scalar, w_pairs[1], w1a, 0, 0, SPLIT)
-        cast(on_scalar, w_pairs[1], w1b, SPLIT, 0, 256)
-        cast(on_vector, w_pairs[1], w1b, SPLIT, 256, N - SPLIT)
-        second = w1a[:, :, 0:CHUNK].bitcast(U32)
-        gather_words(second, 1, 0)
-        x_q1 = keep.tile([P, 2 * S], BF16, name="x_q1", tag="w1b", align_bytes=64)
-        weave(on_scalar, U32, x_q1[:], x_words[:, :, S // 2 : S])
-        gather_words(second, 1, 1)
-        weave(on_scalar, U32, w_q[1], second)
-        gather_words(first, 0, 1)
-        gather_words(third, 2, 1)
-        weave(on_scalar, U32, w_q[2], third)
+        chunk0 = w_woven[0].bitcast(U32).rearrange("p (c u) -> p c u", u=2).rearrange("p c u -> p u c")
+        chunk2 = by_pair(keep.tile([P, 4 * CHUNK], BF16, name="chunk2")[:])
+        gather_words(chunk0, 0, 0)
+        quantise(x_codes[0], x_scales[:, 0:HALF], x_woven0)
+        gather_words(chunk2, 2, 0)
+        chunk3 = by_pair(slots[:, 0 : 2 * CHUNK])
+        gather_words(chunk3, 3, 0)
+
+        cast(on_scalar, w_pairs[1], w1a, 0, 0, PIECE)
+        cast(on_scalar, w_pairs[1], w1b, PIECE, 0, W1_ON_SCALAR)
+        cast(on_vector, w_pairs[1], w1b, PIECE, W1_ON_SCALAR, PIECE)
+        chunk1 = w1a[:, :, 0:CHUNK].bitcast(U32)
+        gather_words(chunk1, 1, 0)
+        x_woven1 = keep.tile([P, 2 * S], BF16, name="x_woven1", tag="w1b", align_bytes=64)
+        weave(on_scalar, U32, x_woven1[:], x_words[:, :, HALF:S])
+        gather_words(chunk1, 1, 1)
+        weave(on_scalar, U32, w_woven[1], chunk1)
+        gather_words(chunk0, 0, 1)
+        gather_words(chunk2, 2, 1)
+        weave(on_scalar, U32, w_woven[2], chunk2)
         quantise_words(0)
         quantise_words(1)
-        quantise(x_codes[1], x_scales[:, S // 2 : S], x_q1[:])
-        gather_words(fourth, 3, 1)
+        quantise(x_codes[1], x_scales[:, HALF:S], x_woven1[:])
+        gather_words(chunk3, 3, 1)
         quantise_words(2)
-        weave(on_vector, I32, w_q[3], fourth)
+        weave(on_vector, I32, w_woven[3], chunk3)
         quantise_words(3)
 
         results = [
-            keep.tile([P, S], F32, name=f"result{c}", tag="w_q3" if c == 2 else f"result{c}", align_bytes=64)
+            keep.tile([P, S], F32, name=f"result{c}", tag="w_woven3" if c == 2 else f"result{c}", align_bytes=64)
             for c in range(CHUNKS)
         ]
-        pieces = [(0, 0, 128), (0, 128, 256), (1, 0, 256), (0, 256, 512), (1, 256, 512)]
+        pieces = [(0, 0, QUARTER), (0, QUARTER, HALF), (1, 0, HALF), (0, HALF, S), (1, HALF, S)]
         pieces = pieces + [(c, j0, j1) for c in (2, 3) for j0, j1 in halves]
         for n, (c, j0, j1) in enumerate(pieces):
             rows = slice(CHUNK * c, CHUNK * (c + 1))
-            acc = psum.tile([P, j1 - j0], F32, name=f"acc{n}", tag=f"bank{(n + 1) % 8}")
+            acc = psum.tile([P, j1 - j0], F32, name=f"acc{n}", tag=f"bank{(n + 1) % BANKS}")
             nc.tensor.matmul_mx(
                 out=acc[:],
                 lhsT=w_codes[:, rows].bitcast(FP8X4),
                 lhsT_scale=w_scales[:, rows],
-                rhs=x_codes[j0 // 256][:, j0 % 256 : j0 % 256 + j1 - j0].bitcast(FP8X4),
+                rhs=x_codes[j0 // HALF][:, j0 % HALF : j0 % HALF + j1 - j0].bitcast(FP8X4),
                 rhs_scale=x_scales[:, j0:j1],
                 start=True,
                 stop=True,
             )
             result = results[c][:, j0:j1]
-            if c >= 2 and j1 == S:
+            late_chunk = c >= 2
+            if late_chunk and j1 == S:
                 nc.vector.tensor_scalar(result, acc[:], bias[:, c : c + 1], None, op0=ADD)
             else:
                 nc.scalar.activation(result, acc[:], IDENTITY, bias=bias[:, c : c + 1])
-            if c < 2 and j1 % 256 == 0:
-                nc.sync.dma_start(out=out[rows, j1 - 256 : j1], in_=results[c][:, j1 - 256 : j1])
-            if c >= 2 and j1 == S:
+            if not late_chunk and j1 % HALF == 0:
+                nc.sync.dma_start(out=out[rows, j1 - HALF : j1], in_=results[c][:, j1 - HALF : j1])
+            if late_chunk and j1 == S:
                 nc.sync.dma_start(out=out[rows, :], in_=results[c][:])

@@ -5,7 +5,6 @@ from concourse.masks import make_identity
 
 F32 = mybir.dt.float32
 BF16 = mybir.dt.bfloat16
-I32 = mybir.dt.int32
 U16 = mybir.dt.uint16
 U32 = mybir.dt.uint32
 U8 = mybir.dt.uint8
@@ -16,20 +15,13 @@ ADD = mybir.AluOpType.add
 
 P = 128
 K, T, S, V, N = 512, 1024, 512, 512, 1024
+PLANES = 4
 CHUNK = 128
 CHUNKS = V // CHUNK
 HALF = S // 2
 QUARTER = S // 4
-PIECE = N // 2
 BANKS = 8
 FLOPS = 2 * K * S * V
-
-X0_ON_SCALAR = 336
-X1_ON_SCALAR = 368
-W0_ON_SCALAR = 320
-W1_ON_SCALAR = 208
-W0_EARLY = 320
-SHARED = 64
 
 
 def tile_picked_cross_bias_l_kernel(tc, xT, w, b, offs, pos1, out):
@@ -42,132 +34,92 @@ def tile_picked_cross_bias_l_kernel(tc, xT, w, b, offs, pos1, out):
         offs_t = lists.tile([P, S // 16], U16, name="offs_t")
         pos1_t = lists.tile([P, V // 16], U16, name="pos1_t")
 
-        x_rows = xT.rearrange("(p u e) n -> p u e n", u=2, e=2)
-        w_rows = w.rearrange("(p u e) n -> p u e n", u=2, e=2)
+        x_rows = xT.rearrange("(p t) n -> p t n", t=PLANES)
+        w_rows = w.rearrange("(p t) n -> p t n", t=PLANES)
 
-        def load(rows, u, name, c0, c1):
-            raw = keep.tile([P, 2, c1 - c0], F32, name=name, tag=name, align_bytes=64)
-            nc.sync.dma_start(out=raw[:], in_=rows[:, u, :, c0:c1])
+        def load(rows, t, name):
+            raw = keep.tile([P, T], F32, name=name, align_bytes=64)
+            nc.sync.dma_start(out=raw[:], in_=rows[:, t, :])
             return raw
 
-        x0 = load(x_rows, 0, "x0", 0, T)
-        nc.sync.dma_start(out=offs_t[:], in_=offs)
-        x1 = load(x_rows, 1, "x1", 0, T)
-        front = S - SHARED
-        stage = keep.tile([P, front + 2 * N], F32, name="stage", align_bytes=64)
-        w0 = stage[:, front:].rearrange("p (e n) -> p e n", e=2)
-        w0_run = w.rearrange("(p u e) n -> p u (e n)", u=2, e=2)[:, 0, :]
-        cut = N + W0_EARLY
-        nc.sync.dma_start(out=stage[:, front : front + cut], in_=w0_run[:, 0:cut])
-        nc.sync.dma_start(out=stage[:, front + cut :], in_=w0_run[:, cut:])
-        nc.sync.dma_start(out=pos1_t[:], in_=pos1)
-        slots = keep.tile([P, CHUNK + 2 * PIECE], F32, name="slots", align_bytes=64)
-        w1a = slots[:, CHUNK:].rearrange("p (e n) -> p e n", e=2)
-        nc.sync.dma_start(out=w1a, in_=w_rows[:, 1, :, 0:PIECE])
-        w1b = load(w_rows, 1, "w1b", PIECE, N)
-
+        b_rows = keep.tile([P, P], F32, name="b_rows")
         ident = keep.tile([P, P], F32, name="ident")
         make_identity(nc, ident[:])
-        b_rows = keep.tile([P, P], F32, name="b_rows")
-        nc.scalar.activation(b_rows[:], ident[:], COPY, scale=0.0)
-        nc.sync.dma_start(out=b_rows[0:CHUNKS, :], in_=b.rearrange("(c p) o -> c (p o)", p=P))
+        nc.vector.memset(b_rows[0 : P - CHUNKS, 0 : P // 2], 0.0)
+        nc.scalar.activation(b_rows[0 : P - CHUNKS, P // 2 : P], b_rows[0 : P - CHUNKS, 0 : P // 2], COPY)
+        x = [load(x_rows, 0, "x0")]
+        nc.sync.dma_start(out=offs_t[:], in_=offs)
+        nc.sync.dma_start(out=b_rows[P - CHUNKS : P, :], in_=b.rearrange("(c p) o -> c (p o)", p=P))
+        x = x + [load(x_rows, t, f"x{t}") for t in range(1, PLANES)]
+        wr = [load(w_rows, 0, "w0")]
+        nc.sync.dma_start(out=pos1_t[:], in_=pos1)
+        wr = wr + [load(w_rows, t, f"w{t}") for t in range(1, PLANES)]
+
         b_turned = psum.tile([P, P], F32, name="b_turned", tag="bank0")
         nc.tensor.transpose(b_turned[:], b_rows[:], ident[:])
         bias = keep.tile([P, CHUNKS], F32, name="bias")
-        nc.scalar.copy(out=bias[:], in_=b_turned[:, 0:CHUNKS])
+        nc.vector.tensor_copy(out=bias[:], in_=b_turned[:, P - CHUNKS : P])
 
-        x_pairs = [keep.tile([P, 2 * T], BF16, name=f"x_pairs{u}") for u in range(2)]
-        w_pairs = [keep.tile([P, 2 * N], BF16, name=f"w_pairs{u}") for u in range(2)]
-        x_woven0 = stage[:, 0:S].bitcast(BF16)
-        x_scales = keep.tile([P, S], U8, name="x_scales", align_bytes=64)
-        w_codes = keep.tile([P, V], U32, name="w_codes", align_bytes=64)
-        w_scales = keep.tile([P, V], U8, name="w_scales", align_bytes=64)
+        def woven_tile(name, cols, tag=None):
+            return keep.tile([P, PLANES * cols], BF16, name=name, tag=tag or name, align_bytes=64)
 
-        on_vector, on_scalar = nc.vector.tensor_copy, nc.scalar.copy
+        def gather_woven(dst, t, raw, offsets, j0, j1):
+            view = dst[:].rearrange("p (c t) -> p t c", t=PLANES)[:, t, :]
+            nc.vector.tensor_copy(view, raw[:].indirect(offsets[:, j0 // 16 : j1 // 16]))
 
-        def cast(copy, pairs, raw, base, c0, c1):
-            copy(
-                out=pairs[:, 2 * (base + c0) : 2 * (base + c1)].rearrange("p (c i e) -> p c e i", i=4, e=2),
-                in_=raw[:, :, c0:c1].rearrange("p e (c i) -> p c e i", i=4),
-            )
+        def gather_run(dst, raw, offsets, j0, j1):
+            nc.scalar.activation(dst, raw[:].indirect(offsets[:, j0 // 16 : j1 // 16]), COPY)
 
-        def gather(dst, pairs, offsets, j0, j1):
-            nc.vector.tensor_copy(dst, pairs[:].bitcast(U32).indirect(offsets[:, j0 // 16 : j1 // 16]))
-
-        def by_pair(ap):
-            return ap.bitcast(U32).rearrange("p (u c) -> p u c", u=2)
-
-        def weave(copy, dtype, dst, src):
-            copy(
-                out=dst.bitcast(dtype).rearrange("p (c i u) -> p c u i", i=2, u=2),
-                in_=src.bitcast(dtype).rearrange("p u (c i) -> p c u i", i=2),
+        def weave(dst, runs, c0, c1):
+            nc.vector.tensor_copy(
+                out=dst[:].rearrange("p (c i t) -> p c t i", i=4, t=PLANES),
+                in_=runs[:].rearrange("p (t c) -> p t c", t=PLANES)[:, :, c0:c1].rearrange("p t (c i) -> p c t i", i=4),
             )
 
         def quantise(codes, scales, src):
             nc.vector.quantize_mx(out=codes.bitcast(FP8X4), scales=scales, in_=src)
 
-        x_words = by_pair(keep.tile([P, 4 * S], BF16, name="x_words")[:])
-        cast(on_scalar, x_pairs[0], x0, 0, 0, X0_ON_SCALAR)
-        cast(on_vector, x_pairs[0], x0, 0, X0_ON_SCALAR, T)
-        gather(x_words[:, 0, :], x_pairs[0], offs_t, 0, S)
-        cast(on_scalar, x_pairs[1], x1, 0, 0, X1_ON_SCALAR)
-        cast(on_vector, x_pairs[1], x1, 0, X1_ON_SCALAR, T)
-        halves = [(0, HALF), (HALF, S)]
-        for j0, j1 in halves:
-            gather(x_words[:, 1, j0:j1], x_pairs[1], offs_t, j0, j1)
+        x_woven = [woven_tile(f"x_woven{h}", HALF) for h in range(2)]
+        x_runs = keep.tile([P, PLANES * HALF], BF16, name="x_runs", align_bytes=64)
+        x_codes = keep.tile([P, S], U32, name="x_codes", align_bytes=64)
+        x_scales = keep.tile([P, S], U8, name="x_scales", align_bytes=64)
+        for t in range(PLANES):
+            gather_run(x_runs[:, t * HALF : (t + 1) * HALF], x[t], offs_t, HALF, S)
+            gather_woven(x_woven[0], t, x[t], offs_t, 0, HALF)
+        weave(x_woven[1], x_runs, 0, HALF)
+        for h in range(2):
+            cols = slice(h * HALF, (h + 1) * HALF)
+            quantise(x_codes[:, cols], x_scales[:, cols], x_woven[h][:])
 
-        cast(on_scalar, w_pairs[0], w0, 0, 0, W0_EARLY)
-        cast(on_scalar, w_pairs[0], w0, 0, W0_EARLY, W0_EARLY + W0_ON_SCALAR)
-        cast(on_vector, w_pairs[0], w0, 0, W0_EARLY + W0_ON_SCALAR, N)
-        weave(on_vector, I32, x_woven0, x_words[:, :, 0:HALF])
-        x_codes = [keep.tile([P, HALF], U32, name=f"x_codes{h}", align_bytes=64)[:] for h in range(2)]
-
-        w_woven = [
-            keep.tile([P, 4 * CHUNK], BF16, name=f"w_woven{c}", tag=f"w_woven{c}", align_bytes=64)[:]
-            for c in range(CHUNKS)
-        ]
-
-        def gather_words(dst, c, u):
-            gather(dst[:, u, :], w_pairs[u], pos1_t, CHUNK * c, CHUNK * (c + 1))
+        rest = V - CHUNK
+        w_woven = [woven_tile(f"w_woven{c}", CHUNK) for c in range(CHUNKS)]
+        w_runs = keep.tile([P, PLANES * rest], BF16, name="w_runs", align_bytes=64)
+        w_codes = keep.tile([P, V], U32, name="w_codes", align_bytes=64)
+        w_scales = keep.tile([P, V], U8, name="w_scales", align_bytes=64)
+        last = PLANES - 1
+        for t in range(last):
+            gather_run(w_runs[:, t * rest : (t + 1) * rest], wr[t], pos1_t, CHUNK, V)
+            gather_woven(w_woven[0], t, wr[t], pos1_t, 0, CHUNK)
+        for c in range(1, CHUNKS):
+            base = last * rest + (c - 1) * CHUNK
+            gather_run(w_runs[:, base : base + CHUNK], wr[last], pos1_t, c * CHUNK, (c + 1) * CHUNK)
+        gather_woven(w_woven[0], last, wr[last], pos1_t, 0, CHUNK)
 
         def quantise_words(c):
             picked = slice(CHUNK * c, CHUNK * (c + 1))
-            quantise(w_codes[:, picked], w_scales[:, picked], w_woven[c])
+            quantise(w_codes[:, picked], w_scales[:, picked], w_woven[c][:])
 
-        chunk0 = w_woven[0].bitcast(U32).rearrange("p (c u) -> p c u", u=2).rearrange("p c u -> p u c")
-        chunk2 = by_pair(keep.tile([P, 4 * CHUNK], BF16, name="chunk2")[:])
-        gather_words(chunk0, 0, 0)
-        quantise(x_codes[0], x_scales[:, 0:HALF], x_woven0)
-        gather_words(chunk2, 2, 0)
-        chunk3 = by_pair(slots[:, 0 : 2 * CHUNK])
-        gather_words(chunk3, 3, 0)
-
-        cast(on_scalar, w_pairs[1], w1a, 0, 0, PIECE)
-        cast(on_scalar, w_pairs[1], w1b, PIECE, 0, W1_ON_SCALAR)
-        cast(on_vector, w_pairs[1], w1b, PIECE, W1_ON_SCALAR, PIECE)
-        chunk1 = w1a[:, :, 0:CHUNK].bitcast(U32)
-        gather_words(chunk1, 1, 0)
-        x_woven1 = keep.tile([P, 2 * S], BF16, name="x_woven1", tag="w1b", align_bytes=64)
-        weave(on_scalar, U32, x_woven1[:], x_words[:, :, HALF:S])
-        gather_words(chunk1, 1, 1)
-        weave(on_scalar, U32, w_woven[1], chunk1)
-        gather_words(chunk0, 0, 1)
-        gather_words(chunk2, 2, 1)
-        weave(on_scalar, U32, w_woven[2], chunk2)
-        quantise_words(0)
-        quantise_words(1)
-        quantise(x_codes[1], x_scales[:, HALF:S], x_woven1[:])
-        gather_words(chunk3, 3, 1)
-        quantise_words(2)
-        weave(on_vector, I32, w_woven[3], chunk3)
-        quantise_words(3)
+        for c in range(1, CHUNKS):
+            weave(w_woven[c], w_runs, (c - 1) * CHUNK, c * CHUNK)
+            quantise_words(c - 1)
+        quantise_words(CHUNKS - 1)
 
         results = [
             keep.tile([P, S], F32, name=f"result{c}", tag="w_woven3" if c == 2 else f"result{c}", align_bytes=64)
             for c in range(CHUNKS)
         ]
-        pieces = [(0, 0, QUARTER), (0, QUARTER, HALF), (1, 0, HALF), (0, HALF, S), (1, HALF, S)]
-        pieces = pieces + [(c, j0, j1) for c in (2, 3) for j0, j1 in halves]
+        halves = [(0, HALF), (HALF, S)]
+        pieces = [(c, j0, j1) for c in range(CHUNKS) for j0, j1 in halves]
         for n, (c, j0, j1) in enumerate(pieces):
             rows = slice(CHUNK * c, CHUNK * (c + 1))
             acc = psum.tile([P, j1 - j0], F32, name=f"acc{n}", tag=f"bank{(n + 1) % BANKS}")
@@ -175,7 +127,7 @@ def tile_picked_cross_bias_l_kernel(tc, xT, w, b, offs, pos1, out):
                 out=acc[:],
                 lhsT=w_codes[:, rows].bitcast(FP8X4),
                 lhsT_scale=w_scales[:, rows],
-                rhs=x_codes[j0 // HALF][:, j0 % HALF : j0 % HALF + j1 - j0].bitcast(FP8X4),
+                rhs=x_codes[:, j0:j1].bitcast(FP8X4),
                 rhs_scale=x_scales[:, j0:j1],
                 start=True,
                 stop=True,
@@ -186,7 +138,7 @@ def tile_picked_cross_bias_l_kernel(tc, xT, w, b, offs, pos1, out):
                 nc.vector.tensor_scalar(result, acc[:], bias[:, c : c + 1], None, op0=ADD)
             else:
                 nc.scalar.activation(result, acc[:], IDENTITY, bias=bias[:, c : c + 1])
-            if not late_chunk and j1 % HALF == 0:
-                nc.sync.dma_start(out=out[rows, j1 - HALF : j1], in_=results[c][:, j1 - HALF : j1])
+            if not late_chunk:
+                nc.sync.dma_start(out=out[rows, j0:j1], in_=result)
             if late_chunk and j1 == S:
                 nc.sync.dma_start(out=out[rows, :], in_=results[c][:])

@@ -34,23 +34,27 @@ def tile_picked_cross_bias_l_kernel(tc, xT, w, b, offs, pos1, out):
         offs_t = lists.tile([P, S // 16], U16, name="offs_t")
         pos1_t = lists.tile([P, V // 16], U16, name="pos1_t")
 
-        x_rows = xT.rearrange("(p t) n -> p t n", t=PLANES)
         w_rows = w.rearrange("(p t) n -> p t n", t=PLANES)
 
         def load(rows, t, name):
             raw = keep.tile([P, T], F32, name=name, align_bytes=64)
             nc.sync.dma_start(out=raw[:], in_=rows[:, t, :])
-            return raw
+            return raw[:]
 
         b_rows = keep.tile([P, P], F32, name="b_rows")
         ident = keep.tile([P, P], F32, name="ident")
         make_identity(nc, ident[:])
         nc.vector.memset(b_rows[0 : P - CHUNKS, 0 : P // 2], 0.0)
         nc.scalar.activation(b_rows[0 : P - CHUNKS, P // 2 : P], b_rows[0 : P - CHUNKS, 0 : P // 2], COPY)
-        x = [load(x_rows, 0, "x0")]
+        nc.scalar.dma_start(out=b_rows[P - CHUNKS : P, :], in_=b.rearrange("(c p) o -> c (p o)", p=P))
+        def load_pair(src, u, name):
+            raw = keep.tile([P, 2 * T], F32, name=name, align_bytes=64)
+            nc.sync.dma_start(out=raw[:], in_=src.rearrange("(p u e) n -> p u (e n)", u=2, e=2)[:, u, :])
+            return [raw[:, 0:T], raw[:, T : 2 * T]]
+
+        x = load_pair(xT, 0, "x01")
         nc.sync.dma_start(out=offs_t[:], in_=offs)
-        nc.sync.dma_start(out=b_rows[P - CHUNKS : P, :], in_=b.rearrange("(c p) o -> c (p o)", p=P))
-        x = x + [load(x_rows, t, f"x{t}") for t in range(1, PLANES)]
+        x = x + load_pair(xT, 1, "x23")
         wr = [load(w_rows, 0, "w0")]
         nc.sync.dma_start(out=pos1_t[:], in_=pos1)
         wr = wr + [load(w_rows, t, f"w{t}") for t in range(1, PLANES)]
@@ -65,34 +69,35 @@ def tile_picked_cross_bias_l_kernel(tc, xT, w, b, offs, pos1, out):
 
         def gather_woven(dst, t, raw, offsets, j0, j1):
             view = dst[:].rearrange("p (c t) -> p t c", t=PLANES)[:, t, :]
-            nc.vector.tensor_copy(view, raw[:].indirect(offsets[:, j0 // 16 : j1 // 16]))
+            nc.vector.tensor_copy(view, raw.indirect(offsets[:, j0 // 16 : j1 // 16]))
 
         def gather_run(dst, raw, offsets, j0, j1):
-            nc.scalar.activation(dst, raw[:].indirect(offsets[:, j0 // 16 : j1 // 16]), COPY)
+            nc.scalar.activation(dst, raw.indirect(offsets[:, j0 // 16 : j1 // 16]), COPY)
 
-        def weave(dst, runs, c0, c1):
+        def weave(dst, runs, c0, c1, t0=0, t1=PLANES):
             nc.vector.tensor_copy(
-                out=dst[:].rearrange("p (c i t) -> p c t i", i=4, t=PLANES),
-                in_=runs[:].rearrange("p (t c) -> p t c", t=PLANES)[:, :, c0:c1].rearrange("p t (c i) -> p c t i", i=4),
+                out=dst[:].rearrange("p (c i t) -> p c t i", i=4, t=PLANES)[:, :, t0:t1, :],
+                in_=runs[:].rearrange("p (t c) -> p t c", t=PLANES)[:, t0:t1, c0:c1].rearrange("p t (c i) -> p c t i", i=4),
             )
 
         def quantise(codes, scales, src):
             nc.vector.quantize_mx(out=codes.bitcast(FP8X4), scales=scales, in_=src)
 
         x_woven = [woven_tile(f"x_woven{h}", HALF) for h in range(2)]
-        x_runs = keep.tile([P, PLANES * HALF], BF16, name="x_runs", align_bytes=64)
+        x_runs = keep.tile([P, PLANES * HALF], F32, name="x_runs", align_bytes=64)
         x_codes = keep.tile([P, S], U32, name="x_codes", align_bytes=64)
         x_scales = keep.tile([P, S], U8, name="x_scales", align_bytes=64)
         for t in range(PLANES):
             gather_run(x_runs[:, t * HALF : (t + 1) * HALF], x[t], offs_t, HALF, S)
             gather_woven(x_woven[0], t, x[t], offs_t, 0, HALF)
-        weave(x_woven[1], x_runs, 0, HALF)
+            if t % 2 == 1:
+                weave(x_woven[1], x_runs, 0, HALF, t - 1, t + 1)
         for h in range(2):
             cols = slice(h * HALF, (h + 1) * HALF)
             quantise(x_codes[:, cols], x_scales[:, cols], x_woven[h][:])
 
         rest = V - CHUNK
-        w_woven = [woven_tile(f"w_woven{c}", CHUNK) for c in range(CHUNKS)]
+        w_woven = [woven_tile(f"w_woven{c}", CHUNK) for c in range(CHUNKS - 1)]
         w_runs = keep.tile([P, PLANES * rest], BF16, name="w_runs", align_bytes=64)
         w_codes = keep.tile([P, V], U32, name="w_codes", align_bytes=64)
         w_scales = keep.tile([P, V], U8, name="w_scales", align_bytes=64)
@@ -100,6 +105,9 @@ def tile_picked_cross_bias_l_kernel(tc, xT, w, b, offs, pos1, out):
         for t in range(last):
             gather_run(w_runs[:, t * rest : (t + 1) * rest], wr[t], pos1_t, CHUNK, V)
             gather_woven(w_woven[0], t, wr[t], pos1_t, 0, CHUNK)
+            if t == 1:
+                for c in range(1, CHUNKS - 1):
+                    weave(w_woven[c], w_runs, (c - 1) * CHUNK, c * CHUNK, 0, 2)
         for c in range(1, CHUNKS):
             base = last * rest + (c - 1) * CHUNK
             gather_run(w_runs[:, base : base + CHUNK], wr[last], pos1_t, c * CHUNK, (c + 1) * CHUNK)
@@ -109,13 +117,20 @@ def tile_picked_cross_bias_l_kernel(tc, xT, w, b, offs, pos1, out):
             picked = slice(CHUNK * c, CHUNK * (c + 1))
             quantise(w_codes[:, picked], w_scales[:, picked], w_woven[c][:])
 
-        for c in range(1, CHUNKS):
-            weave(w_woven[c], w_runs, (c - 1) * CHUNK, c * CHUNK)
-            quantise_words(c - 1)
-        quantise_words(CHUNKS - 1)
+        def weave_late(c):
+            weave(w_woven[c], w_runs, (c - 1) * CHUNK, c * CHUNK, 2, PLANES)
+
+        quantise_words(0)
+        weave_late(1)
+        weave_late(2)
+        quantise_words(1)
+        quantise_words(2)
+        w_woven.append(woven_tile("w_woven3", CHUNK, tag="w_woven1"))
+        weave(w_woven[3], w_runs, 2 * CHUNK, 3 * CHUNK)
+        quantise_words(3)
 
         results = [
-            keep.tile([P, S], F32, name=f"result{c}", tag="w_woven3" if c == 2 else f"result{c}", align_bytes=64)
+            keep.tile([P, S], F32, name=f"result{c}", tag="w_woven1" if c == 2 else f"result{c}", align_bytes=64)
             for c in range(CHUNKS)
         ]
         halves = [(0, HALF), (HALF, S)]

@@ -34,6 +34,7 @@ def tile_picked_cross_bias_l_kernel(tc, xT, w, b, offs, pos1, out):
         offs_t = lists.tile([P, S // 16], U16, name="offs_t")
         pos1_t = lists.tile([P, V // 16], U16, name="pos1_t")
 
+        x_rows = xT.rearrange("(p t) n -> p t n", t=PLANES)
         w_rows = w.rearrange("(p t) n -> p t n", t=PLANES)
 
         def load(rows, t, name):
@@ -54,7 +55,7 @@ def tile_picked_cross_bias_l_kernel(tc, xT, w, b, offs, pos1, out):
 
         x = load_pair(xT, 0, "x01")
         nc.sync.dma_start(out=offs_t[:], in_=offs)
-        x = x + load_pair(xT, 1, "x23")
+        x = x + [load(x_rows, t, f"x{t}") for t in range(2, PLANES)]
         wr = [load(w_rows, 0, "w0")]
         nc.sync.dma_start(out=pos1_t[:], in_=pos1)
         wr = wr + [load(w_rows, t, f"w{t}") for t in range(1, PLANES)]
@@ -68,7 +69,7 @@ def tile_picked_cross_bias_l_kernel(tc, xT, w, b, offs, pos1, out):
             return keep.tile([P, PLANES * cols], BF16, name=name, tag=tag or name, align_bytes=64)
 
         def gather_woven(dst, t, raw, offsets, j0, j1):
-            view = dst[:].rearrange("p (c t) -> p t c", t=PLANES)[:, t, :]
+            view = dst.rearrange("p (c t) -> p t c", t=PLANES)[:, t, :]
             nc.vector.tensor_copy(view, raw.indirect(offsets[:, j0 // 16 : j1 // 16]))
 
         def gather_run(dst, raw, offsets, j0, j1):
@@ -76,14 +77,14 @@ def tile_picked_cross_bias_l_kernel(tc, xT, w, b, offs, pos1, out):
 
         def weave(dst, runs, c0, c1, t0=0, t1=PLANES):
             nc.vector.tensor_copy(
-                out=dst[:].rearrange("p (c i t) -> p c t i", i=4, t=PLANES)[:, :, t0:t1, :],
+                out=dst.rearrange("p (c i t) -> p c t i", i=4, t=PLANES)[:, :, t0:t1, :],
                 in_=runs[:].rearrange("p (t c) -> p t c", t=PLANES)[:, t0:t1, c0:c1].rearrange("p t (c i) -> p c t i", i=4),
             )
 
         def quantise(codes, scales, src):
             nc.vector.quantize_mx(out=codes.bitcast(FP8X4), scales=scales, in_=src)
 
-        x_woven = [woven_tile(f"x_woven{h}", HALF) for h in range(2)]
+        x_woven = [woven_tile(f"x_woven{h}", HALF)[:] for h in range(2)]
         x_runs = keep.tile([P, PLANES * HALF], F32, name="x_runs", align_bytes=64)
         x_codes = keep.tile([P, S], U32, name="x_codes", align_bytes=64)
         x_scales = keep.tile([P, S], U8, name="x_scales", align_bytes=64)
@@ -94,20 +95,29 @@ def tile_picked_cross_bias_l_kernel(tc, xT, w, b, offs, pos1, out):
                 weave(x_woven[1], x_runs, 0, HALF, t - 1, t + 1)
         for h in range(2):
             cols = slice(h * HALF, (h + 1) * HALF)
-            quantise(x_codes[:, cols], x_scales[:, cols], x_woven[h][:])
+            quantise(x_codes[:, cols], x_scales[:, cols], x_woven[h])
 
         rest = V - CHUNK
-        w_woven = [woven_tile(f"w_woven{c}", CHUNK) for c in range(CHUNKS - 1)]
+        w_woven0 = keep.tile([P, PLANES * CHUNK], BF16, name="w_woven0", tag="x_runs", align_bytes=64)
+        w_woven12 = woven_tile("w_woven12", 2 * CHUNK)
+        first, second = w_woven12[:, 0 : PLANES * CHUNK], w_woven12[:, PLANES * CHUNK : 2 * PLANES * CHUNK]
+        w_woven = [w_woven0[:], first, second, first]
         w_runs = keep.tile([P, PLANES * rest], BF16, name="w_runs", align_bytes=64)
         w_codes = keep.tile([P, V], U32, name="w_codes", align_bytes=64)
         w_scales = keep.tile([P, V], U8, name="w_scales", align_bytes=64)
         last = PLANES - 1
-        for t in range(last):
-            gather_run(w_runs[:, t * rest : (t + 1) * rest], wr[t], pos1_t, CHUNK, V)
-            gather_woven(w_woven[0], t, wr[t], pos1_t, 0, CHUNK)
-            if t == 1:
-                for c in range(1, CHUNKS - 1):
-                    weave(w_woven[c], w_runs, (c - 1) * CHUNK, c * CHUNK, 0, 2)
+
+        def gather_words(t, c0, c1):
+            gather_run(w_runs[:, t * rest + (c0 - 1) * CHUNK : t * rest + (c1 - 1) * CHUNK], wr[t], pos1_t, c0 * CHUNK, c1 * CHUNK)
+
+        gather_words(0, 1, 4)
+        gather_woven(w_woven[0], 0, wr[0], pos1_t, 0, CHUNK)
+        gather_words(1, 1, 3)
+        gather_words(1, 3, 4)
+        gather_woven(w_woven[0], 1, wr[1], pos1_t, 0, CHUNK)
+        weave(w_woven12[:], w_runs, 0, 2 * CHUNK, 0, 2)
+        gather_words(2, 1, 4)
+        gather_woven(w_woven[0], 2, wr[2], pos1_t, 0, CHUNK)
         for c in range(1, CHUNKS):
             base = last * rest + (c - 1) * CHUNK
             gather_run(w_runs[:, base : base + CHUNK], wr[last], pos1_t, c * CHUNK, (c + 1) * CHUNK)
@@ -115,7 +125,7 @@ def tile_picked_cross_bias_l_kernel(tc, xT, w, b, offs, pos1, out):
 
         def quantise_words(c):
             picked = slice(CHUNK * c, CHUNK * (c + 1))
-            quantise(w_codes[:, picked], w_scales[:, picked], w_woven[c][:])
+            quantise(w_codes[:, picked], w_scales[:, picked], w_woven[c])
 
         def weave_late(c):
             weave(w_woven[c], w_runs, (c - 1) * CHUNK, c * CHUNK, 2, PLANES)
@@ -125,12 +135,11 @@ def tile_picked_cross_bias_l_kernel(tc, xT, w, b, offs, pos1, out):
         weave_late(2)
         quantise_words(1)
         quantise_words(2)
-        w_woven.append(woven_tile("w_woven3", CHUNK, tag="w_woven1"))
         weave(w_woven[3], w_runs, 2 * CHUNK, 3 * CHUNK)
         quantise_words(3)
 
         results = [
-            keep.tile([P, S], F32, name=f"result{c}", tag="w_woven1" if c == 2 else f"result{c}", align_bytes=64)
+            keep.tile([P, S], F32, name=f"result{c}", tag="w_woven12" if c == 2 else f"result{c}", align_bytes=64)
             for c in range(CHUNKS)
         ]
         halves = [(0, HALF), (HALF, S)]

@@ -75,10 +75,16 @@ def tile_picked_cross_bias_l_kernel(tc, xT, w, b, offs, pos1, out):
         def gather_run(dst, raw, offsets, j0, j1):
             nc.scalar.activation(dst, raw.indirect(offsets[:, j0 // 16 : j1 // 16]), COPY)
 
-        def weave(dst, runs, c0, c1, t0=0, t1=PLANES):
+        def weave(dst, runs, c0, c1):
             nc.vector.tensor_copy(
-                out=dst.rearrange("p (c i t) -> p c t i", i=4, t=PLANES)[:, :, t0:t1, :],
-                in_=runs[:].rearrange("p (t c) -> p t c", t=PLANES)[:, t0:t1, c0:c1].rearrange("p t (c i) -> p c t i", i=4),
+                out=dst.rearrange("p (c i t) -> p c t i", i=4, t=PLANES),
+                in_=runs[:].rearrange("p (t c) -> p t c", t=PLANES)[:, :, c0:c1].rearrange("p t (c i) -> p c t i", i=4),
+            )
+
+        def weave_pair(dst, runs, c0, c1, t0):
+            nc.vector.tensor_copy(
+                out=dst.rearrange("p (c t) -> p c t", t=PLANES)[:, :, t0 : t0 + 2],
+                in_=runs[:].rearrange("p (t c) -> p c t", t=PLANES)[:, c0:c1, t0 : t0 + 2],
             )
 
         def quantise(codes, scales, src):
@@ -92,7 +98,7 @@ def tile_picked_cross_bias_l_kernel(tc, xT, w, b, offs, pos1, out):
             gather_run(x_runs[:, t * HALF : (t + 1) * HALF], x[t], offs_t, HALF, S)
             gather_woven(x_woven[0], t, x[t], offs_t, 0, HALF)
             if t % 2 == 1:
-                weave(x_woven[1], x_runs, 0, HALF, t - 1, t + 1)
+                weave_pair(x_woven[1], x_runs, 0, HALF, t - 1)
         for h in range(2):
             cols = slice(h * HALF, (h + 1) * HALF)
             quantise(x_codes[:, cols], x_scales[:, cols], x_woven[h])
@@ -115,7 +121,7 @@ def tile_picked_cross_bias_l_kernel(tc, xT, w, b, offs, pos1, out):
         gather_words(1, 1, 3)
         gather_words(1, 3, 4)
         gather_woven(w_woven[0], 1, wr[1], pos1_t, 0, CHUNK)
-        weave(w_woven12[:], w_runs, 0, 2 * CHUNK, 0, 2)
+        weave_pair(w_woven12[:], w_runs, 0, 2 * CHUNK, 0)
         gather_words(2, 1, 4)
         gather_woven(w_woven[0], 2, wr[2], pos1_t, 0, CHUNK)
         for c in range(1, CHUNKS):
@@ -128,7 +134,7 @@ def tile_picked_cross_bias_l_kernel(tc, xT, w, b, offs, pos1, out):
             quantise(w_codes[:, picked], w_scales[:, picked], w_woven[c])
 
         def weave_late(c):
-            weave(w_woven[c], w_runs, (c - 1) * CHUNK, c * CHUNK, 2, PLANES)
+            weave_pair(w_woven[c], w_runs, (c - 1) * CHUNK, c * CHUNK, 2)
 
         quantise_words(0)
         weave_late(1)
@@ -142,9 +148,18 @@ def tile_picked_cross_bias_l_kernel(tc, xT, w, b, offs, pos1, out):
             keep.tile([P, S], F32, name=f"result{c}", tag="w_woven12" if c == 2 else f"result{c}", align_bytes=64)
             for c in range(CHUNKS)
         ]
-        halves = [(0, HALF), (HALF, S)]
-        pieces = [(c, j0, j1) for c in range(CHUNKS) for j0, j1 in halves]
-        for n, (c, j0, j1) in enumerate(pieces):
+        def on_scalar(result, acc, c):
+            nc.scalar.activation(result, acc, IDENTITY, bias=bias[:, c : c + 1])
+
+        def on_vector(result, acc, c):
+            nc.vector.tensor_scalar(result, acc, bias[:, c : c + 1], None, op0=ADD)
+
+        q3 = HALF + QUARTER
+        pieces = [(0, 0, QUARTER, on_scalar), (0, QUARTER, HALF, on_scalar), (0, HALF, S, on_scalar)]
+        pieces = pieces + [(1, 0, HALF, on_scalar), (1, HALF, S, on_scalar)]
+        pieces = pieces + [(2, 0, HALF, on_vector), (2, HALF, q3, on_scalar), (2, q3, S, on_vector)]
+        pieces = pieces + [(3, 0, HALF, on_scalar), (3, HALF, q3, on_vector), (3, q3, S, on_scalar)]
+        for n, (c, j0, j1, empty) in enumerate(pieces):
             rows = slice(CHUNK * c, CHUNK * (c + 1))
             acc = psum.tile([P, j1 - j0], F32, name=f"acc{n}", tag=f"bank{(n + 1) % BANKS}")
             nc.tensor.matmul_mx(
@@ -156,13 +171,9 @@ def tile_picked_cross_bias_l_kernel(tc, xT, w, b, offs, pos1, out):
                 start=True,
                 stop=True,
             )
-            result = results[c][:, j0:j1]
+            empty(results[c][:, j0:j1], acc[:], c)
             late_chunk = c >= 2
-            if late_chunk and j1 == S:
-                nc.vector.tensor_scalar(result, acc[:], bias[:, c : c + 1], None, op0=ADD)
-            else:
-                nc.scalar.activation(result, acc[:], IDENTITY, bias=bias[:, c : c + 1])
-            if not late_chunk:
-                nc.sync.dma_start(out=out[rows, j0:j1], in_=result)
+            if not late_chunk and j1 % HALF == 0:
+                nc.sync.dma_start(out=out[rows, j1 - HALF : j1], in_=results[c][:, j1 - HALF : j1])
             if late_chunk and j1 == S:
                 nc.sync.dma_start(out=out[rows, :], in_=results[c][:])

@@ -47,15 +47,10 @@ def tile_picked_cross_bias_l_kernel(tc, xT, w, b, offs, pos1, out):
         make_identity(nc, ident[:])
         nc.vector.memset(b_rows[0 : P - CHUNKS, 0 : P // 2], 0.0)
         nc.scalar.activation(b_rows[0 : P - CHUNKS, P // 2 : P], b_rows[0 : P - CHUNKS, 0 : P // 2], COPY)
-        nc.scalar.dma_start(out=b_rows[P - CHUNKS : P, :], in_=b.rearrange("(c p) o -> c (p o)", p=P))
-        def load_pair(src, u, name):
-            raw = keep.tile([P, 2 * T], F32, name=name, align_bytes=64)
-            nc.sync.dma_start(out=raw[:], in_=src.rearrange("(p u e) n -> p u (e n)", u=2, e=2)[:, u, :])
-            return [raw[:, 0:T], raw[:, T : 2 * T]]
-
-        x = load_pair(xT, 0, "x01")
+        nc.gpsimd.dma_start(out=b_rows[P - CHUNKS : P, :], in_=b.rearrange("(c p) o -> c (p o)", p=P))
+        x = [load(x_rows, 0, "x0")]
         nc.sync.dma_start(out=offs_t[:], in_=offs)
-        x = x + [load(x_rows, t, f"x{t}") for t in range(2, PLANES)]
+        x = x + [load(x_rows, t, f"x{t}") for t in range(1, PLANES)]
         wr = [load(w_rows, 0, "w0")]
         nc.sync.dma_start(out=pos1_t[:], in_=pos1)
         wr = wr + [load(w_rows, t, f"w{t}") for t in range(1, PLANES)]

@@ -85,18 +85,30 @@ def tile_picked_cross_bias_l_kernel(tc, xT, w, b, offs, pos1, out):
         def quantise(codes, scales, src):
             nc.vector.quantize_mx(out=codes.bitcast(FP8X4), scales=scales, in_=src)
 
-        x_woven = [woven_tile(f"x_woven{h}", HALF)[:] for h in range(2)]
-        x_runs = keep.tile([P, PLANES * HALF], F32, name="x_runs", align_bytes=64)
+        far = S - QUARTER
+        x_woven = woven_tile("x_woven", S)
+        x_runs = keep.tile([P, PLANES * far], F32, name="x_runs", align_bytes=64)
         x_codes = keep.tile([P, S], U32, name="x_codes", align_bytes=64)
         x_scales = keep.tile([P, S], U8, name="x_scales", align_bytes=64)
-        for t in range(PLANES):
-            gather_run(x_runs[:, t * HALF : (t + 1) * HALF], x[t], offs_t, HALF, S)
-            gather_woven(x_woven[0], t, x[t], offs_t, 0, HALF)
-            if t % 2 == 1:
-                weave_pair(x_woven[1], x_runs, 0, HALF, t - 1)
+
+        def gather_tokens(t, j0, j1):
+            gather_run(x_runs[:, t * far + j0 - QUARTER : t * far + j1 - QUARTER], x[t], offs_t, j0, j1)
+
+        def weave_tokens(t0, j0, j1):
+            weave_pair(x_woven[:, PLANES * j0 : PLANES * j1], x_runs, j0 - QUARTER, j1 - QUARTER, t0)
+
+        for t in range(PLANES - 1):
+            gather_tokens(t, QUARTER, S)
+            gather_woven(x_woven[:, 0 : PLANES * QUARTER], t, x[t], offs_t, 0, QUARTER)
+            if t == 1:
+                weave_tokens(0, QUARTER, S)
+        gather_woven(x_woven[:, 0 : PLANES * QUARTER], PLANES - 1, x[PLANES - 1], offs_t, 0, QUARTER)
+        for j0, j1 in [(QUARTER, HALF), (HALF, S)]:
+            gather_tokens(PLANES - 1, j0, j1)
+            weave_tokens(2, j0, j1)
         for h in range(2):
             cols = slice(h * HALF, (h + 1) * HALF)
-            quantise(x_codes[:, cols], x_scales[:, cols], x_woven[h])
+            quantise(x_codes[:, cols], x_scales[:, cols], x_woven[:, PLANES * h * HALF : PLANES * (h + 1) * HALF])
 
         rest = V - CHUNK
         w_woven0 = keep.tile([P, PLANES * CHUNK], BF16, name="w_woven0", tag="x_runs", align_bytes=64)

@@ -14,8 +14,9 @@ IDENTITY = mybir.ActivationFunctionType.Identity
 ADD = mybir.AluOpType.add
 
 P = 128
-K, T, S, V, N = 512, 1024, 512, 512, 1024
+K, T, S, V = 512, 1024, 512, 512
 PLANES = 4
+PER_COLUMN = 16
 CHUNK = 128
 CHUNKS = V // CHUNK
 HALF = S // 2
@@ -31,123 +32,133 @@ def tile_picked_cross_bias_l_kernel(tc, xT, w, b, offs, pos1, out):
         keep = ctx.enter_context(tc.tile_pool(name="keep", bufs=1))
         psum = ctx.enter_context(tc.psum_pool(name="psum", bufs=1))
 
-        offs_t = lists.tile([P, S // 16], U16, name="offs_t")
-        pos1_t = lists.tile([P, V // 16], U16, name="pos1_t")
+        offs_t = lists.tile([P, S // PER_COLUMN], U16, name="offs_t")
+        pos1_t = lists.tile([P, V // PER_COLUMN], U16, name="pos1_t")
 
         x_rows = xT.rearrange("(p t) n -> p t n", t=PLANES)
         w_rows = w.rearrange("(p t) n -> p t n", t=PLANES)
 
         def load(rows, t, name):
-            raw = keep.tile([P, T], F32, name=name, align_bytes=64)
-            nc.sync.dma_start(out=raw[:], in_=rows[:, t, :])
-            return raw[:]
+            plane = keep.tile([P, T], F32, name=name, align_bytes=64)
+            nc.sync.dma_start(out=plane[:], in_=rows[:, t, :])
+            return plane[:]
 
+        spare = P - CHUNKS
         b_rows = keep.tile([P, P], F32, name="b_rows")
         ident = keep.tile([P, P], F32, name="ident")
         make_identity(nc, ident[:])
-        nc.vector.memset(b_rows[0 : P - CHUNKS, 0 : P // 2], 0.0)
-        nc.scalar.activation(b_rows[0 : P - CHUNKS, P // 2 : P], b_rows[0 : P - CHUNKS, 0 : P // 2], COPY)
-        nc.gpsimd.dma_start(out=b_rows[P - CHUNKS : P, :], in_=b.rearrange("(c p) o -> c (p o)", p=P))
-        x = [load(x_rows, 0, "x0")]
+        nc.vector.memset(b_rows[0:spare, 0 : P // 2], 0.0)
+        nc.scalar.activation(b_rows[0:spare, P // 2 : P], b_rows[0:spare, 0 : P // 2], COPY)
+
+        x01 = keep.tile([P, 2 * T], F32, name="x01", align_bytes=64)
+        nc.sync.dma_start(out=x01[:], in_=xT.rearrange("(p u e) n -> p u (e n)", u=2, e=2)[:, 0, :])
         nc.sync.dma_start(out=offs_t[:], in_=offs)
-        x = x + [load(x_rows, t, f"x{t}") for t in range(1, PLANES)]
-        wr = [load(w_rows, 0, "w0")]
+        nc.sync.dma_start(out=b_rows[spare:P, :], in_=b.rearrange("(c p) o -> c (p o)", p=P))
+        x_planes = [x01[:, 0:T], x01[:, T : 2 * T]] + [load(x_rows, t, f"x{t}") for t in range(2, PLANES)]
+        w_planes = [load(w_rows, 0, "w0")]
         nc.sync.dma_start(out=pos1_t[:], in_=pos1)
-        wr = wr + [load(w_rows, t, f"w{t}") for t in range(1, PLANES)]
+        w_planes = w_planes + [load(w_rows, t, f"w{t}") for t in range(1, PLANES)]
 
         b_turned = psum.tile([P, P], F32, name="b_turned", tag="bank0")
         nc.tensor.transpose(b_turned[:], b_rows[:], ident[:])
         bias = keep.tile([P, CHUNKS], F32, name="bias")
-        nc.vector.tensor_copy(out=bias[:], in_=b_turned[:, P - CHUNKS : P])
+        nc.vector.tensor_copy(out=bias[:], in_=b_turned[:, spare:P])
 
-        def woven_tile(name, cols, tag=None):
-            return keep.tile([P, PLANES * cols], BF16, name=name, tag=tag or name, align_bytes=64)
+        def woven_tile(name, columns):
+            return keep.tile([P, PLANES * columns], BF16, name=name, align_bytes=64)
 
-        def gather_woven(dst, t, raw, offsets, j0, j1):
-            view = dst.rearrange("p (c t) -> p t c", t=PLANES)[:, t, :]
-            nc.vector.tensor_copy(view, raw.indirect(offsets[:, j0 // 16 : j1 // 16]))
+        def looked_up(plane, offsets, j0, j1):
+            return plane.indirect(offsets[:, j0 // PER_COLUMN : j1 // PER_COLUMN])
 
-        def gather_run(dst, raw, offsets, j0, j1):
-            nc.scalar.activation(dst, raw.indirect(offsets[:, j0 // 16 : j1 // 16]), COPY)
+        def gather_woven(woven, t, plane, offsets, j0, j1):
+            places = woven.rearrange("p (c t) -> p t c", t=PLANES)[:, t, :]
+            nc.vector.tensor_copy(places, looked_up(plane, offsets, j0, j1))
 
-        def weave(dst, runs, c0, c1):
+        def gather_run(run, plane, offsets, j0, j1):
+            nc.scalar.activation(run, looked_up(plane, offsets, j0, j1), COPY)
+
+        def weave(woven, runs, c0, c1):
             nc.vector.tensor_copy(
-                out=dst.rearrange("p (c i t) -> p c t i", i=4, t=PLANES),
+                out=woven.rearrange("p (c i t) -> p c t i", i=4, t=PLANES),
                 in_=runs[:].rearrange("p (t c) -> p t c", t=PLANES)[:, :, c0:c1].rearrange("p t (c i) -> p c t i", i=4),
             )
 
-        def weave_pair(dst, runs, c0, c1, t0):
+        def weave_pair(woven, runs, c0, c1, t0):
             nc.vector.tensor_copy(
-                out=dst.rearrange("p (c t) -> p c t", t=PLANES)[:, :, t0 : t0 + 2],
+                out=woven.rearrange("p (c t) -> p c t", t=PLANES)[:, :, t0 : t0 + 2],
                 in_=runs[:].rearrange("p (t c) -> p c t", t=PLANES)[:, c0:c1, t0 : t0 + 2],
             )
 
-        def quantise(codes, scales, src):
-            nc.vector.quantize_mx(out=codes.bitcast(FP8X4), scales=scales, in_=src)
+        def quantise(codes, scales, woven):
+            nc.vector.quantize_mx(out=codes.bitcast(FP8X4), scales=scales, in_=woven)
 
-        far = S - QUARTER
+        in_runs = S - QUARTER
         x_woven = woven_tile("x_woven", S)
-        x_runs = keep.tile([P, PLANES * far], F32, name="x_runs", align_bytes=64)
+        x_runs = keep.tile([P, PLANES * in_runs], F32, name="x_runs", align_bytes=64)
         x_codes = keep.tile([P, S], U32, name="x_codes", align_bytes=64)
         x_scales = keep.tile([P, S], U8, name="x_scales", align_bytes=64)
+        first_quarter = x_woven[:, 0 : PLANES * QUARTER]
+
+        def token_run(t, j0, j1):
+            return x_runs[:, t * in_runs + j0 - QUARTER : t * in_runs + j1 - QUARTER]
 
         def gather_tokens(t, j0, j1):
-            gather_run(x_runs[:, t * far + j0 - QUARTER : t * far + j1 - QUARTER], x[t], offs_t, j0, j1)
+            gather_run(token_run(t, j0, j1), x_planes[t], offs_t, j0, j1)
 
         def weave_tokens(t0, j0, j1):
             weave_pair(x_woven[:, PLANES * j0 : PLANES * j1], x_runs, j0 - QUARTER, j1 - QUARTER, t0)
 
-        for t in range(PLANES - 1):
-            gather_tokens(t, QUARTER, S)
-            gather_woven(x_woven[:, 0 : PLANES * QUARTER], t, x[t], offs_t, 0, QUARTER)
-            if t == 1:
-                weave_tokens(0, QUARTER, S)
-        gather_woven(x_woven[:, 0 : PLANES * QUARTER], PLANES - 1, x[PLANES - 1], offs_t, 0, QUARTER)
+        for t in range(2):
+            gather_tokens(t, HALF, S)
+            gather_woven(first_quarter, t, x_planes[t], offs_t, 0, QUARTER)
+            nc.vector.tensor_copy(token_run(t, QUARTER, HALF), looked_up(x_planes[t], offs_t, QUARTER, HALF))
+        gather_tokens(2, QUARTER, S)
+        gather_woven(first_quarter, 2, x_planes[2], offs_t, 0, QUARTER)
+        weave_tokens(0, QUARTER, S)
+        gather_woven(first_quarter, 3, x_planes[3], offs_t, 0, QUARTER)
         for j0, j1 in [(QUARTER, HALF), (HALF, S)]:
-            gather_tokens(PLANES - 1, j0, j1)
+            gather_tokens(3, j0, j1)
             weave_tokens(2, j0, j1)
-        for h in range(2):
-            cols = slice(h * HALF, (h + 1) * HALF)
-            quantise(x_codes[:, cols], x_scales[:, cols], x_woven[:, PLANES * h * HALF : PLANES * (h + 1) * HALF])
+        for j0 in (0, HALF):
+            tokens = slice(j0, j0 + HALF)
+            quantise(x_codes[:, tokens], x_scales[:, tokens], x_woven[:, PLANES * j0 : PLANES * (j0 + HALF)])
 
-        rest = V - CHUNK
+        run_width = V - CHUNK
         w_woven0 = keep.tile([P, PLANES * CHUNK], BF16, name="w_woven0", tag="x_runs", align_bytes=64)
         w_woven12 = woven_tile("w_woven12", 2 * CHUNK)
-        first, second = w_woven12[:, 0 : PLANES * CHUNK], w_woven12[:, PLANES * CHUNK : 2 * PLANES * CHUNK]
-        w_woven = [w_woven0[:], first, second, first]
-        w_runs = keep.tile([P, PLANES * rest], BF16, name="w_runs", align_bytes=64)
+        place1, place2 = w_woven12[:, 0 : PLANES * CHUNK], w_woven12[:, PLANES * CHUNK : 2 * PLANES * CHUNK]
+        w_woven = [w_woven0[:], place1, place2, place1]
+        w_runs = keep.tile([P, PLANES * run_width], BF16, name="w_runs", align_bytes=64)
         w_codes = keep.tile([P, V], U32, name="w_codes", align_bytes=64)
         w_scales = keep.tile([P, V], U8, name="w_scales", align_bytes=64)
-        last = PLANES - 1
 
         def gather_words(t, c0, c1):
-            gather_run(w_runs[:, t * rest + (c0 - 1) * CHUNK : t * rest + (c1 - 1) * CHUNK], wr[t], pos1_t, c0 * CHUNK, c1 * CHUNK)
+            run = w_runs[:, t * run_width + (c0 - 1) * CHUNK : t * run_width + (c1 - 1) * CHUNK]
+            gather_run(run, w_planes[t], pos1_t, c0 * CHUNK, c1 * CHUNK)
 
-        gather_words(0, 1, 4)
-        gather_woven(w_woven[0], 0, wr[0], pos1_t, 0, CHUNK)
-        gather_words(1, 1, 3)
-        gather_words(1, 3, 4)
-        gather_woven(w_woven[0], 1, wr[1], pos1_t, 0, CHUNK)
-        weave_pair(w_woven12[:], w_runs, 0, 2 * CHUNK, 0)
-        gather_words(2, 1, 4)
-        gather_woven(w_woven[0], 2, wr[2], pos1_t, 0, CHUNK)
-        for c in range(1, CHUNKS):
-            base = last * rest + (c - 1) * CHUNK
-            gather_run(w_runs[:, base : base + CHUNK], wr[last], pos1_t, c * CHUNK, (c + 1) * CHUNK)
-        gather_woven(w_woven[0], last, wr[last], pos1_t, 0, CHUNK)
+        def gather_chunk0(t):
+            gather_woven(w_woven[0], t, w_planes[t], pos1_t, 0, CHUNK)
 
         def quantise_words(c):
-            picked = slice(CHUNK * c, CHUNK * (c + 1))
-            quantise(w_codes[:, picked], w_scales[:, picked], w_woven[c])
+            words = slice(CHUNK * c, CHUNK * (c + 1))
+            quantise(w_codes[:, words], w_scales[:, words], w_woven[c])
 
-        def weave_late(c):
-            weave_pair(w_woven[c], w_runs, (c - 1) * CHUNK, c * CHUNK, 2)
-
+        gather_words(0, 1, CHUNKS)
+        gather_chunk0(0)
+        gather_words(1, 1, 3)
+        gather_words(1, 3, CHUNKS)
+        gather_chunk0(1)
+        weave_pair(w_woven12[:], w_runs, 0, 2 * CHUNK, 0)
+        gather_words(2, 1, CHUNKS)
+        gather_chunk0(2)
+        for c in range(1, CHUNKS):
+            gather_words(3, c, c + 1)
+        gather_chunk0(3)
         quantise_words(0)
-        weave_late(1)
-        weave_late(2)
-        quantise_words(1)
-        quantise_words(2)
+        for c in (1, 2):
+            weave_pair(w_woven[c], w_runs, (c - 1) * CHUNK, c * CHUNK, 2)
+        for c in (1, 2):
+            quantise_words(c)
         weave(w_woven[3], w_runs, 2 * CHUNK, 3 * CHUNK)
         quantise_words(3)
 
@@ -155,17 +166,18 @@ def tile_picked_cross_bias_l_kernel(tc, xT, w, b, offs, pos1, out):
             keep.tile([P, S], F32, name=f"result{c}", tag="w_woven12" if c == 2 else f"result{c}", align_bytes=64)
             for c in range(CHUNKS)
         ]
+
         def on_scalar(result, acc, c):
             nc.scalar.activation(result, acc, IDENTITY, bias=bias[:, c : c + 1])
 
         def on_vector(result, acc, c):
             nc.vector.tensor_scalar(result, acc, bias[:, c : c + 1], None, op0=ADD)
 
-        q3 = HALF + QUARTER
+        last_quarter = S - QUARTER
         pieces = [(0, 0, QUARTER, on_scalar), (0, QUARTER, HALF, on_scalar), (0, HALF, S, on_scalar)]
         pieces = pieces + [(1, 0, HALF, on_scalar), (1, HALF, S, on_scalar)]
-        pieces = pieces + [(2, 0, HALF, on_vector), (2, HALF, q3, on_scalar), (2, q3, S, on_vector)]
-        pieces = pieces + [(3, 0, HALF, on_scalar), (3, HALF, q3, on_vector), (3, q3, S, on_scalar)]
+        pieces = pieces + [(2, 0, HALF, on_vector), (2, HALF, last_quarter, on_scalar), (2, last_quarter, S, on_vector)]
+        pieces = pieces + [(3, 0, HALF, on_scalar), (3, HALF, last_quarter, on_vector), (3, last_quarter, S, on_scalar)]
         for n, (c, j0, j1, empty) in enumerate(pieces):
             rows = slice(CHUNK * c, CHUNK * (c + 1))
             acc = psum.tile([P, j1 - j0], F32, name=f"acc{n}", tag=f"bank{(n + 1) % BANKS}")

@@ -1,7 +1,6 @@
 from contextlib import ExitStack
 
 import concourse.mybir as mybir
-from concourse.masks import make_identity
 
 F32 = mybir.dt.float32
 BF16 = mybir.dt.bfloat16
@@ -43,26 +42,21 @@ def tile_picked_cross_bias_l_kernel(tc, xT, w, b, offs, pos1, out):
             nc.sync.dma_start(out=plane[:], in_=rows[:, t, :])
             return plane[:]
 
-        spare = P - CHUNKS
-        b_rows = keep.tile([P, P], F32, name="b_rows")
-        ident = keep.tile([P, P], F32, name="ident")
-        make_identity(nc, ident[:])
-        nc.vector.memset(b_rows[0:spare, 0 : P // 2], 0.0)
-        nc.scalar.activation(b_rows[0:spare, P // 2 : P], b_rows[0:spare, 0 : P // 2], COPY)
+        warm = keep.tile([P, 2], F32, name="warm")
+        nc.vector.memset(warm[:, 0:1], 0.0)
+        nc.scalar.activation(warm[:, 1:2], warm[:, 0:1], COPY)
 
         x01 = keep.tile([P, 2 * T], F32, name="x01", align_bytes=64)
         nc.sync.dma_start(out=x01[:], in_=xT.rearrange("(p u e) n -> p u (e n)", u=2, e=2)[:, 0, :])
         nc.sync.dma_start(out=offs_t[:], in_=offs)
-        nc.sync.dma_start(out=b_rows[spare:P, :], in_=b.rearrange("(c p) o -> c (p o)", p=P))
         x_planes = [x01[:, 0:T], x01[:, T : 2 * T]] + [load(x_rows, t, f"x{t}") for t in range(2, PLANES)]
         w_planes = [load(w_rows, 0, "w0")]
         nc.sync.dma_start(out=pos1_t[:], in_=pos1)
         w_planes = w_planes + [load(w_rows, t, f"w{t}") for t in range(1, PLANES)]
 
-        b_turned = psum.tile([P, P], F32, name="b_turned", tag="bank0")
-        nc.tensor.transpose(b_turned[:], b_rows[:], ident[:])
         bias = keep.tile([P, CHUNKS], F32, name="bias")
-        nc.vector.tensor_copy(out=bias[:], in_=b_turned[:, spare:P])
+        with nc.allow_non_contiguous_dma(reason="one bias value a partition and chunk"):
+            nc.sync.dma_start(out=bias[:], in_=b.rearrange("(c p) o -> p (c o)", p=P))
 
         def woven_tile(name, columns):
             return keep.tile([P, PLANES * columns], BF16, name=name, align_bytes=64)

@@ -21,6 +21,7 @@ CHUNKS = V // CHUNK
 HALF = S // 2
 QUARTER = S // 4
 BANKS = 8
+IN_PLACE = 192
 FLOPS = 2 * K * S * V
 
 
@@ -34,32 +35,24 @@ def tile_picked_cross_bias_l_kernel(tc, xT, w, b, offs, pos1, out):
         offs_t = lists.tile([P, S // PER_COLUMN], U16, name="offs_t")
         pos1_t = lists.tile([P, V // PER_COLUMN], U16, name="pos1_t")
 
-        x_rows = xT.rearrange("(p t) n -> p t n", t=PLANES)
-        w_rows = w.rearrange("(p t) n -> p t n", t=PLANES)
-
-        def load(rows, t, name):
-            plane = keep.tile([P, T], F32, name=name, align_bytes=64)
-            nc.sync.dma_start(out=plane[:], in_=rows[:, t, :])
-            return plane[:]
+        def load(matrix, t0, t1, name):
+            tile = keep.tile([P, (t1 - t0) * T], F32, name=name, align_bytes=64)
+            nc.sync.dma_start(out=tile[:], in_=matrix.rearrange("(p t) n -> p (t n)", t=PLANES)[:, t0 * T : t1 * T])
+            return [tile[:, i * T : (i + 1) * T] for i in range(t1 - t0)]
 
         warm = keep.tile([P, 2], F32, name="warm")
         nc.vector.memset(warm[:, 0:1], 0.0)
         nc.scalar.activation(warm[:, 1:2], warm[:, 0:1], COPY)
 
-        x01 = keep.tile([P, 2 * T], F32, name="x01", align_bytes=64)
-        nc.sync.dma_start(out=x01[:], in_=xT.rearrange("(p u e) n -> p u (e n)", u=2, e=2)[:, 0, :])
+        x_planes = load(xT, 0, 2, "x01")
         nc.sync.dma_start(out=offs_t[:], in_=offs)
-        x_planes = [x01[:, 0:T], x01[:, T : 2 * T]] + [load(x_rows, t, f"x{t}") for t in range(2, PLANES)]
-        w_planes = [load(w_rows, 0, "w0")]
+        x_planes = x_planes + load(xT, 2, 4, "x23")
         nc.sync.dma_start(out=pos1_t[:], in_=pos1)
-        w_planes = w_planes + [load(w_rows, t, f"w{t}") for t in range(1, PLANES)]
+        w_planes = load(w, 0, 2, "w01") + load(w, 2, 3, "w2") + load(w, 3, 4, "w3")
 
         bias = keep.tile([P, CHUNKS], F32, name="bias")
         with nc.allow_non_contiguous_dma(reason="one bias value a partition and chunk"):
             nc.sync.dma_start(out=bias[:], in_=b.rearrange("(c p) o -> p (c o)", p=P))
-
-        def woven_tile(name, columns):
-            return keep.tile([P, PLANES * columns], BF16, name=name, align_bytes=64)
 
         def looked_up(plane, offsets, j0, j1):
             return plane.indirect(offsets[:, j0 // PER_COLUMN : j1 // PER_COLUMN])
@@ -86,49 +79,50 @@ def tile_picked_cross_bias_l_kernel(tc, xT, w, b, offs, pos1, out):
         def quantise(codes, scales, woven):
             nc.vector.quantize_mx(out=codes.bitcast(FP8X4), scales=scales, in_=woven)
 
-        in_runs = S - QUARTER
-        x_woven = woven_tile("x_woven", S)
+        in_runs = S - IN_PLACE
+        x_woven = keep.tile([P, PLANES * S], BF16, name="x_woven", align_bytes=64)
         x_runs = keep.tile([P, PLANES * in_runs], F32, name="x_runs", align_bytes=64)
         x_codes = keep.tile([P, S], U32, name="x_codes", align_bytes=64)
         x_scales = keep.tile([P, S], U8, name="x_scales", align_bytes=64)
-        first_quarter = x_woven[:, 0 : PLANES * QUARTER]
-
-        def token_run(t, j0, j1):
-            return x_runs[:, t * in_runs + j0 - QUARTER : t * in_runs + j1 - QUARTER]
+        in_place = x_woven[:, 0 : PLANES * IN_PLACE]
 
         def gather_tokens(t, j0, j1):
-            gather_run(token_run(t, j0, j1), x_planes[t], offs_t, j0, j1)
+            run = x_runs[:, t * in_runs + j0 - IN_PLACE : t * in_runs + j1 - IN_PLACE]
+            gather_run(run, x_planes[t], offs_t, j0, j1)
 
         def weave_tokens(t0, j0, j1):
-            weave_pair(x_woven[:, PLANES * j0 : PLANES * j1], x_runs, j0 - QUARTER, j1 - QUARTER, t0)
+            weave_pair(x_woven[:, PLANES * j0 : PLANES * j1], x_runs, j0 - IN_PLACE, j1 - IN_PLACE, t0)
 
         for t in range(2):
-            gather_tokens(t, HALF, S)
-            gather_woven(first_quarter, t, x_planes[t], offs_t, 0, QUARTER)
-            nc.vector.tensor_copy(token_run(t, QUARTER, HALF), looked_up(x_planes[t], offs_t, QUARTER, HALF))
-        gather_tokens(2, QUARTER, S)
-        gather_woven(first_quarter, 2, x_planes[2], offs_t, 0, QUARTER)
-        weave_tokens(0, QUARTER, S)
-        gather_woven(first_quarter, 3, x_planes[3], offs_t, 0, QUARTER)
-        for j0, j1 in [(QUARTER, HALF), (HALF, S)]:
-            gather_tokens(3, j0, j1)
+            gather_tokens(t, IN_PLACE, S)
+            gather_woven(in_place, t, x_planes[t], offs_t, 0, IN_PLACE)
+        weave_tokens(0, IN_PLACE, S)
+        for t in range(2, PLANES):
+            gather_woven(in_place, t, x_planes[t], offs_t, 0, IN_PLACE)
+        for j0, j1 in [(IN_PLACE, IN_PLACE + CHUNK), (IN_PLACE + CHUNK, IN_PLACE + 2 * CHUNK), (IN_PLACE + 2 * CHUNK, S)]:
+            for t in range(2, PLANES):
+                gather_tokens(t, j0, j1)
             weave_tokens(2, j0, j1)
         for j0 in (0, HALF):
             tokens = slice(j0, j0 + HALF)
             quantise(x_codes[:, tokens], x_scales[:, tokens], x_woven[:, PLANES * j0 : PLANES * (j0 + HALF)])
 
-        run_width = V - CHUNK
-        w_woven0 = keep.tile([P, PLANES * CHUNK], BF16, name="w_woven0", tag="x_runs", align_bytes=64)
-        w_woven12 = woven_tile("w_woven12", 2 * CHUNK)
+        pitch = 2 * CHUNK
+        runs12 = keep.tile([P, PLANES * pitch], F32, name="runs12", align_bytes=64)
+        runs3 = keep.tile([P, PLANES * pitch], F32, name="runs3", align_bytes=64)
+        w_woven12 = keep.tile([P, 2 * PLANES * CHUNK], BF16, name="w_woven12", align_bytes=64)
         place1, place2 = w_woven12[:, 0 : PLANES * CHUNK], w_woven12[:, PLANES * CHUNK : 2 * PLANES * CHUNK]
-        w_woven = [w_woven0[:], place1, place2, place1]
-        w_runs = keep.tile([P, PLANES * run_width], BF16, name="w_runs", align_bytes=64)
+        w_woven = [runs3[:, 2 * pitch : 3 * pitch].bitcast(BF16), place1, place2, place1]
         w_codes = keep.tile([P, V], U32, name="w_codes", align_bytes=64)
         w_scales = keep.tile([P, V], U8, name="w_scales", align_bytes=64)
 
+        def word_run(t, c0, c1):
+            if c0 == 3:
+                return runs3[:, t * pitch : t * pitch + CHUNK]
+            return runs12[:, t * pitch + (c0 - 1) * CHUNK : t * pitch + (c1 - 1) * CHUNK]
+
         def gather_words(t, c0, c1):
-            run = w_runs[:, t * run_width + (c0 - 1) * CHUNK : t * run_width + (c1 - 1) * CHUNK]
-            gather_run(run, w_planes[t], pos1_t, c0 * CHUNK, c1 * CHUNK)
+            gather_run(word_run(t, c0, c1), w_planes[t], pos1_t, c0 * CHUNK, c1 * CHUNK)
 
         def gather_chunk0(t):
             gather_woven(w_woven[0], t, w_planes[t], pos1_t, 0, CHUNK)
@@ -137,23 +131,25 @@ def tile_picked_cross_bias_l_kernel(tc, xT, w, b, offs, pos1, out):
             words = slice(CHUNK * c, CHUNK * (c + 1))
             quantise(w_codes[:, words], w_scales[:, words], w_woven[c])
 
-        gather_words(0, 1, CHUNKS)
-        gather_chunk0(0)
+        gather_words(0, 1, 3)
         gather_words(1, 1, 3)
-        gather_words(1, 3, CHUNKS)
+        gather_words(0, 3, 4)
+        gather_chunk0(0)
         gather_chunk0(1)
-        weave_pair(w_woven12[:], w_runs, 0, 2 * CHUNK, 0)
-        gather_words(2, 1, CHUNKS)
+        nc.vector.tensor_copy(word_run(1, 3, 4), looked_up(w_planes[1], pos1_t, 3 * CHUNK, V))
+        weave_pair(w_woven[1], runs12, 0, CHUNK, 0)
+        gather_words(2, 1, 3)
         gather_chunk0(2)
         for c in range(1, CHUNKS):
             gather_words(3, c, c + 1)
         gather_chunk0(3)
         quantise_words(0)
-        for c in (1, 2):
-            weave_pair(w_woven[c], w_runs, (c - 1) * CHUNK, c * CHUNK, 2)
+        gather_words(2, 3, 4)
+        weave_pair(w_woven[1], runs12, 0, CHUNK, 2)
+        weave(w_woven[2], runs12, CHUNK, 2 * CHUNK)
         for c in (1, 2):
             quantise_words(c)
-        weave(w_woven[3], w_runs, 2 * CHUNK, 3 * CHUNK)
+        weave(w_woven[3], runs3, 0, CHUNK)
         quantise_words(3)
 
         results = [

@@ -21,7 +21,8 @@ CHUNKS = V // CHUNK
 HALF = S // 2
 QUARTER = S // 4
 BANKS = 8
-IN_PLACE = 192
+IN_PLACE = 224
+HELD = 64
 FLOPS = 2 * K * S * V
 
 
@@ -48,7 +49,10 @@ def tile_picked_cross_bias_l_kernel(tc, xT, w, b, offs, pos1, out):
         nc.sync.dma_start(out=offs_t[:], in_=offs)
         x_planes = x_planes + load(xT, 2, 4, "x23")
         nc.sync.dma_start(out=pos1_t[:], in_=pos1)
-        w_planes = load(w, 0, 2, "w01") + load(w, 2, 3, "w2") + load(w, 3, 4, "w3")
+        w_all = keep.tile([P, PLANES * T], F32, name="w_all", align_bytes=64)
+        w_rows = w.rearrange("(p t) n -> p (t n)", t=PLANES)
+        for t0, t1 in [(0, 2), (2, 3), (3, 4)]:
+            nc.sync.dma_start(out=w_all[:, t0 * T : t1 * T], in_=w_rows[:, t0 * T : t1 * T])
 
         bias = keep.tile([P, CHUNKS], F32, name="bias")
         with nc.allow_non_contiguous_dma(reason="one bias value a partition and chunk"):
@@ -61,7 +65,7 @@ def tile_picked_cross_bias_l_kernel(tc, xT, w, b, offs, pos1, out):
             places = woven.rearrange("p (c t) -> p t c", t=PLANES)[:, t, :]
             nc.vector.tensor_copy(places, looked_up(plane, offsets, j0, j1))
 
-        def gather_run(run, plane, offsets, j0, j1):
+        def on_scalar_run(run, plane, offsets, j0, j1):
             nc.scalar.activation(run, looked_up(plane, offsets, j0, j1), COPY)
 
         def weave(woven, runs, c0, c1):
@@ -82,13 +86,13 @@ def tile_picked_cross_bias_l_kernel(tc, xT, w, b, offs, pos1, out):
         in_runs = S - IN_PLACE
         x_woven = keep.tile([P, PLANES * S], BF16, name="x_woven", align_bytes=64)
         x_runs = keep.tile([P, PLANES * in_runs], F32, name="x_runs", align_bytes=64)
-        x_codes = keep.tile([P, S], U32, name="x_codes", align_bytes=64)
+        x_codes = keep.tile([P, S], U32, name="x_codes", tag="x23", align_bytes=64)
         x_scales = keep.tile([P, S], U8, name="x_scales", align_bytes=64)
         in_place = x_woven[:, 0 : PLANES * IN_PLACE]
 
         def gather_tokens(t, j0, j1):
             run = x_runs[:, t * in_runs + j0 - IN_PLACE : t * in_runs + j1 - IN_PLACE]
-            gather_run(run, x_planes[t], offs_t, j0, j1)
+            on_scalar_run(run, x_planes[t], offs_t, j0, j1)
 
         def weave_tokens(t0, j0, j1):
             weave_pair(x_woven[:, PLANES * j0 : PLANES * j1], x_runs, j0 - IN_PLACE, j1 - IN_PLACE, t0)
@@ -99,7 +103,7 @@ def tile_picked_cross_bias_l_kernel(tc, xT, w, b, offs, pos1, out):
         weave_tokens(0, IN_PLACE, S)
         for t in range(2, PLANES):
             gather_woven(in_place, t, x_planes[t], offs_t, 0, IN_PLACE)
-        for j0, j1 in [(IN_PLACE, IN_PLACE + CHUNK), (IN_PLACE + CHUNK, IN_PLACE + 2 * CHUNK), (IN_PLACE + 2 * CHUNK, S)]:
+        for j0, j1 in [(IN_PLACE, IN_PLACE + CHUNK), (IN_PLACE + CHUNK, S)]:
             for t in range(2, PLANES):
                 gather_tokens(t, j0, j1)
             weave_tokens(2, j0, j1)
@@ -107,53 +111,45 @@ def tile_picked_cross_bias_l_kernel(tc, xT, w, b, offs, pos1, out):
             tokens = slice(j0, j0 + HALF)
             quantise(x_codes[:, tokens], x_scales[:, tokens], x_woven[:, PLANES * j0 : PLANES * (j0 + HALF)])
 
-        pitch = 2 * CHUNK
-        runs12 = keep.tile([P, PLANES * pitch], F32, name="runs12", align_bytes=64)
-        runs3 = keep.tile([P, PLANES * pitch], F32, name="runs3", align_bytes=64)
-        w_woven12 = keep.tile([P, 2 * PLANES * CHUNK], BF16, name="w_woven12", align_bytes=64)
-        place1, place2 = w_woven12[:, 0 : PLANES * CHUNK], w_woven12[:, PLANES * CHUNK : 2 * PLANES * CHUNK]
-        w_woven = [runs3[:, 2 * pitch : 3 * pitch].bitcast(BF16), place1, place2, place1]
+        w_runs = keep.tile([P, PLANES * V], F32, name="w_runs", align_bytes=64)
+        w_places = keep.tile([P, 3 * PLANES * CHUNK], BF16, name="w_places", align_bytes=64)
+        w_woven = [w_places[:, PLANES * CHUNK * i : PLANES * CHUNK * (i + 1)] for i in (0, 1, 2, 1)]
         w_codes = keep.tile([P, V], U32, name="w_codes", align_bytes=64)
         w_scales = keep.tile([P, V], U8, name="w_scales", align_bytes=64)
 
-        def word_run(t, c0, c1):
-            if c0 == 3:
-                return runs3[:, t * pitch : t * pitch + CHUNK]
-            return runs12[:, t * pitch + (c0 - 1) * CHUNK : t * pitch + (c1 - 1) * CHUNK]
-
-        def gather_words(t, c0, c1):
-            gather_run(word_run(t, c0, c1), w_planes[t], pos1_t, c0 * CHUNK, c1 * CHUNK)
+        def gather_words(t, j0, j1, last_plane):
+            on_scalar_run(w_runs[:, t * V + j0 : t * V + j1], w_all[:, t * T : (last_plane + 1) * T], pos1_t, j0, j1)
 
         def gather_chunk0(t):
-            gather_woven(w_woven[0], t, w_planes[t], pos1_t, 0, CHUNK)
+            gather_woven(w_woven[0], t, w_all[:, t * T : (t + 1) * T], pos1_t, 0, CHUNK)
 
         def quantise_words(c):
             words = slice(CHUNK * c, CHUNK * (c + 1))
             quantise(w_codes[:, words], w_scales[:, words], w_woven[c])
 
-        gather_words(0, 1, 3)
-        gather_words(1, 1, 3)
-        gather_words(0, 3, 4)
+        gather_words(0, CHUNK, 2 * CHUNK, 0)
+        gather_words(1, CHUNK, V - HELD, 1)
+        gather_words(0, 2 * CHUNK, V, 0)
         gather_chunk0(0)
         gather_chunk0(1)
-        nc.vector.tensor_copy(word_run(1, 3, 4), looked_up(w_planes[1], pos1_t, 3 * CHUNK, V))
-        weave_pair(w_woven[1], runs12, 0, CHUNK, 0)
-        gather_words(2, 1, 3)
+        weave_pair(w_woven[1], w_runs, CHUNK, 2 * CHUNK, 0)
+        gather_words(2, CHUNK, 3 * CHUNK, 2)
         gather_chunk0(2)
         for c in range(1, CHUNKS):
-            gather_words(3, c, c + 1)
+            gather_words(3, c * CHUNK, (c + 1) * CHUNK, 3)
+        gather_words(2, 3 * CHUNK, V, 3)
+        gather_words(1, V - HELD, V, 3)
         gather_chunk0(3)
         quantise_words(0)
-        gather_words(2, 3, 4)
-        weave_pair(w_woven[1], runs12, 0, CHUNK, 2)
-        weave(w_woven[2], runs12, CHUNK, 2 * CHUNK)
+        weave_pair(w_woven[1], w_runs, CHUNK, 2 * CHUNK, 2)
+        weave(w_woven[2], w_runs, 2 * CHUNK, 3 * CHUNK)
         for c in (1, 2):
             quantise_words(c)
-        weave(w_woven[3], runs3, 0, CHUNK)
+        weave(w_woven[3], w_runs, 3 * CHUNK, V)
         quantise_words(3)
 
         results = [
-            keep.tile([P, S], F32, name=f"result{c}", tag="w_woven12" if c == 2 else f"result{c}", align_bytes=64)
+            keep.tile([P, S], F32, name=f"result{c}", tag="w_places" if c == 2 else f"result{c}", align_bytes=64)
             for c in range(CHUNKS)
         ]
 

@@ -22,7 +22,6 @@ HALF = S // 2
 QUARTER = S // 4
 BANKS = 8
 IN_PLACE = 224
-HELD = 64
 FLOPS = 2 * K * S * V
 
 
@@ -54,9 +53,13 @@ def tile_picked_cross_bias_l_kernel(tc, xT, w, b, offs, pos1, out):
         for t0, t1 in [(0, 2), (2, 3), (3, 4)]:
             nc.sync.dma_start(out=w_all[:, t0 * T : t1 * T], in_=w_rows[:, t0 * T : t1 * T])
 
-        bias = keep.tile([P, CHUNKS], F32, name="bias")
+        bias0 = keep.tile([P, 1], F32, name="bias0")
+        bias123 = keep.tile([P, CHUNKS - 1], F32, name="bias123")
+        bias = [bias0[:]] + [bias123[:, c : c + 1] for c in range(CHUNKS - 1)]
         with nc.allow_non_contiguous_dma(reason="one bias value a partition and chunk"):
-            nc.sync.dma_start(out=bias[:], in_=b.rearrange("(c p) o -> p (c o)", p=P))
+            columns = b.rearrange("(c p) o -> p (c o)", p=P)
+            nc.sync.dma_start(out=bias0[:], in_=columns[:, 0:1])
+            nc.sync.dma_start(out=bias123[:], in_=columns[:, 1:CHUNKS])
 
         def looked_up(plane, offsets, j0, j1):
             return plane.indirect(offsets[:, j0 // PER_COLUMN : j1 // PER_COLUMN])
@@ -67,6 +70,9 @@ def tile_picked_cross_bias_l_kernel(tc, xT, w, b, offs, pos1, out):
 
         def on_scalar_run(run, plane, offsets, j0, j1):
             nc.scalar.activation(run, looked_up(plane, offsets, j0, j1), COPY)
+
+        def on_vector_run(run, plane, offsets, j0, j1):
+            nc.vector.tensor_copy(run, looked_up(plane, offsets, j0, j1))
 
         def weave(woven, runs, c0, c1):
             nc.vector.tensor_copy(
@@ -117,8 +123,8 @@ def tile_picked_cross_bias_l_kernel(tc, xT, w, b, offs, pos1, out):
         w_codes = keep.tile([P, V], U32, name="w_codes", align_bytes=64)
         w_scales = keep.tile([P, V], U8, name="w_scales", align_bytes=64)
 
-        def gather_words(t, j0, j1, last_plane):
-            on_scalar_run(w_runs[:, t * V + j0 : t * V + j1], w_all[:, t * T : (last_plane + 1) * T], pos1_t, j0, j1)
+        def gather_words(fetch, t, j0, j1, last_plane):
+            fetch(w_runs[:, t * V + j0 : t * V + j1], w_all[:, t * T : (last_plane + 1) * T], pos1_t, j0, j1)
 
         def gather_chunk0(t):
             gather_woven(w_woven[0], t, w_all[:, t * T : (t + 1) * T], pos1_t, 0, CHUNK)
@@ -127,18 +133,17 @@ def tile_picked_cross_bias_l_kernel(tc, xT, w, b, offs, pos1, out):
             words = slice(CHUNK * c, CHUNK * (c + 1))
             quantise(w_codes[:, words], w_scales[:, words], w_woven[c])
 
-        gather_words(0, CHUNK, 2 * CHUNK, 0)
-        gather_words(1, CHUNK, V - HELD, 1)
-        gather_words(0, 2 * CHUNK, V, 0)
-        gather_chunk0(0)
-        gather_chunk0(1)
-        weave_pair(w_woven[1], w_runs, CHUNK, 2 * CHUNK, 0)
-        gather_words(2, CHUNK, 3 * CHUNK, 2)
+        gather_words(on_vector_run, 1, 0, 2 * CHUNK, 1)
+        gather_words(on_vector_run, 1, 2 * CHUNK, 3 * CHUNK, 1)
+        gather_words(on_scalar_run, 0, 0, 2 * CHUNK, 0)
+        gather_words(on_scalar_run, 0, 2 * CHUNK, V, 0)
+        gather_words(on_scalar_run, 1, 3 * CHUNK, V, 1)
+        weave_pair(w_places[:, 0 : 2 * PLANES * CHUNK], w_runs, 0, 2 * CHUNK, 0)
+        gather_words(on_scalar_run, 2, CHUNK, 3 * CHUNK, 2)
         gather_chunk0(2)
         for c in range(1, CHUNKS):
-            gather_words(3, c * CHUNK, (c + 1) * CHUNK, 3)
-        gather_words(2, 3 * CHUNK, V, 3)
-        gather_words(1, V - HELD, V, 3)
+            gather_words(on_scalar_run, 3, c * CHUNK, (c + 1) * CHUNK, 3)
+        gather_words(on_scalar_run, 2, 3 * CHUNK, V, 3)
         gather_chunk0(3)
         quantise_words(0)
         weave_pair(w_woven[1], w_runs, CHUNK, 2 * CHUNK, 2)
@@ -154,10 +159,10 @@ def tile_picked_cross_bias_l_kernel(tc, xT, w, b, offs, pos1, out):
         ]
 
         def on_scalar(result, acc, c):
-            nc.scalar.activation(result, acc, IDENTITY, bias=bias[:, c : c + 1])
+            nc.scalar.activation(result, acc, IDENTITY, bias=bias[c])
 
         def on_vector(result, acc, c):
-            nc.vector.tensor_scalar(result, acc, bias[:, c : c + 1], None, op0=ADD)
+            nc.vector.tensor_scalar(result, acc, bias[c], None, op0=ADD)
 
         last_quarter = S - QUARTER
         pieces = [(0, 0, QUARTER, on_scalar), (0, QUARTER, HALF, on_scalar), (0, HALF, S, on_scalar)]

from contextlib import ExitStack

import concourse.mybir as mybir

F32 = mybir.dt.float32
BF16 = mybir.dt.bfloat16
U16 = mybir.dt.uint16
U32 = mybir.dt.uint32
U8 = mybir.dt.uint8
FP8X4 = mybir.dt.float8_e4m3fn_x4
COPY = mybir.ActivationFunctionType.Copy
IDENTITY = mybir.ActivationFunctionType.Identity
ADD = mybir.AluOpType.add

P = 128
K, T, S, V = 512, 1024, 512, 512
PLANES = 4
PER_COLUMN = 16
CHUNK = 128
CHUNKS = V // CHUNK
HALF = S // 2
QUARTER = S // 4
BANKS = 8
IN_PLACE = 224
FLOPS = 2 * K * S * V


def tile_picked_cross_bias_l_kernel(tc, xT, w, b, offs, pos1, out):
    nc = tc.nc
    with ExitStack() as ctx:
        lists = ctx.enter_context(tc.tile_pool(name="lists", bufs=1))
        keep = ctx.enter_context(tc.tile_pool(name="keep", bufs=1))
        psum = ctx.enter_context(tc.psum_pool(name="psum", bufs=1))

        offs_t = lists.tile([P, S // PER_COLUMN], U16, name="offs_t")
        pos1_t = lists.tile([P, V // PER_COLUMN], U16, name="pos1_t")

        def load(matrix, t0, t1, name):
            tile = keep.tile([P, (t1 - t0) * T], F32, name=name, align_bytes=64)
            nc.sync.dma_start(out=tile[:], in_=matrix.rearrange("(p t) n -> p (t n)", t=PLANES)[:, t0 * T : t1 * T])
            return [tile[:, i * T : (i + 1) * T] for i in range(t1 - t0)]

        warm = keep.tile([P, 2], F32, name="warm")
        nc.vector.memset(warm[:, 0:1], 0.0)
        nc.scalar.activation(warm[:, 1:2], warm[:, 0:1], COPY)

        x_planes = load(xT, 0, 2, "x01")
        nc.sync.dma_start(out=offs_t[:], in_=offs)
        x_planes = x_planes + load(xT, 2, 4, "x23")
        nc.sync.dma_start(out=pos1_t[:], in_=pos1)
        w_all = keep.tile([P, PLANES * T], F32, name="w_all", align_bytes=64)
        w_rows = w.rearrange("(p t) n -> p (t n)", t=PLANES)
        for t0, t1 in [(0, 2), (2, 3), (3, 4)]:
            nc.sync.dma_start(out=w_all[:, t0 * T : t1 * T], in_=w_rows[:, t0 * T : t1 * T])

        bias0 = keep.tile([P, 1], F32, name="bias0")
        bias123 = keep.tile([P, CHUNKS - 1], F32, name="bias123")
        bias = [bias0[:]] + [bias123[:, c : c + 1] for c in range(CHUNKS - 1)]
        with nc.allow_non_contiguous_dma(reason="one bias value a partition and chunk"):
            columns = b.rearrange("(c p) o -> p (c o)", p=P)
            nc.sync.dma_start(out=bias0[:], in_=columns[:, 0:1])
            nc.sync.dma_start(out=bias123[:], in_=columns[:, 1:CHUNKS])

        def looked_up(plane, offsets, j0, j1):
            return plane.indirect(offsets[:, j0 // PER_COLUMN : j1 // PER_COLUMN])

        def gather_woven(woven, t, plane, offsets, j0, j1):
            places = woven.rearrange("p (c t) -> p t c", t=PLANES)[:, t, :]
            nc.vector.tensor_copy(places, looked_up(plane, offsets, j0, j1))

        def on_scalar_run(run, plane, offsets, j0, j1):
            nc.scalar.activation(run, looked_up(plane, offsets, j0, j1), COPY)

        def on_vector_run(run, plane, offsets, j0, j1):
            nc.vector.tensor_copy(run, looked_up(plane, offsets, j0, j1))

        def weave(woven, runs, c0, c1):
            nc.vector.tensor_copy(
                out=woven.rearrange("p (c i t) -> p c t i", i=4, t=PLANES),
                in_=runs[:].rearrange("p (t c) -> p t c", t=PLANES)[:, :, c0:c1].rearrange("p t (c i) -> p c t i", i=4),
            )

        def weave_pair(woven, runs, c0, c1, t0):
            nc.vector.tensor_copy(
                out=woven.rearrange("p (c t) -> p c t", t=PLANES)[:, :, t0 : t0 + 2],
                in_=runs[:].rearrange("p (t c) -> p c t", t=PLANES)[:, c0:c1, t0 : t0 + 2],
            )

        def quantise(codes, scales, woven):
            nc.vector.quantize_mx(out=codes.bitcast(FP8X4), scales=scales, in_=woven)

        in_runs = S - IN_PLACE
        x_woven = keep.tile([P, PLANES * S], BF16, name="x_woven", align_bytes=64)
        x_runs = keep.tile([P, PLANES * in_runs], F32, name="x_runs", align_bytes=64)
        x_codes = keep.tile([P, S], U32, name="x_codes", tag="x23", align_bytes=64)
        x_scales = keep.tile([P, S], U8, name="x_scales", align_bytes=64)
        in_place = x_woven[:, 0 : PLANES * IN_PLACE]

        def gather_tokens(t, j0, j1):
            run = x_runs[:, t * in_runs + j0 - IN_PLACE : t * in_runs + j1 - IN_PLACE]
            on_scalar_run(run, x_planes[t], offs_t, j0, j1)

        def weave_tokens(t0, j0, j1):
            weave_pair(x_woven[:, PLANES * j0 : PLANES * j1], x_runs, j0 - IN_PLACE, j1 - IN_PLACE, t0)

        for t in range(2):
            gather_tokens(t, IN_PLACE, S)
            gather_woven(in_place, t, x_planes[t], offs_t, 0, IN_PLACE)
        weave_tokens(0, IN_PLACE, S)
        for t in range(2, PLANES):
            gather_woven(in_place, t, x_planes[t], offs_t, 0, IN_PLACE)
        for j0, j1 in [(IN_PLACE, IN_PLACE + CHUNK), (IN_PLACE + CHUNK, S)]:
            for t in range(2, PLANES):
                gather_tokens(t, j0, j1)
            weave_tokens(2, j0, j1)
        for j0 in (0, HALF):
            tokens = slice(j0, j0 + HALF)
            quantise(x_codes[:, tokens], x_scales[:, tokens], x_woven[:, PLANES * j0 : PLANES * (j0 + HALF)])

        w_runs = keep.tile([P, PLANES * V], F32, name="w_runs", align_bytes=64)
        w_places = keep.tile([P, 3 * PLANES * CHUNK], BF16, name="w_places", align_bytes=64)
        w_woven = [w_places[:, PLANES * CHUNK * i : PLANES * CHUNK * (i + 1)] for i in (0, 1, 2, 1)]
        w_codes = keep.tile([P, V], U32, name="w_codes", align_bytes=64)
        w_scales = keep.tile([P, V], U8, name="w_scales", align_bytes=64)

        def gather_words(fetch, t, j0, j1, last_plane):
            fetch(w_runs[:, t * V + j0 : t * V + j1], w_all[:, t * T : (last_plane + 1) * T], pos1_t, j0, j1)

        def gather_chunk0(t):
            gather_woven(w_woven[0], t, w_all[:, t * T : (t + 1) * T], pos1_t, 0, CHUNK)

        def quantise_words(c):
            words = slice(CHUNK * c, CHUNK * (c + 1))
            quantise(w_codes[:, words], w_scales[:, words], w_woven[c])

        gather_words(on_vector_run, 1, 0, 2 * CHUNK, 1)
        gather_words(on_vector_run, 1, 2 * CHUNK, 3 * CHUNK, 1)
        gather_words(on_scalar_run, 0, 0, 2 * CHUNK, 0)
        gather_words(on_scalar_run, 0, 2 * CHUNK, V, 0)
        gather_words(on_scalar_run, 1, 3 * CHUNK, V, 1)
        weave_pair(w_places[:, 0 : 2 * PLANES * CHUNK], w_runs, 0, 2 * CHUNK, 0)
        gather_words(on_scalar_run, 2, CHUNK, 3 * CHUNK, 2)
        gather_chunk0(2)
        for c in range(1, CHUNKS):
            gather_words(on_scalar_run, 3, c * CHUNK, (c + 1) * CHUNK, 3)
        gather_words(on_scalar_run, 2, 3 * CHUNK, V, 3)
        gather_chunk0(3)
        quantise_words(0)
        weave_pair(w_woven[1], w_runs, CHUNK, 2 * CHUNK, 2)
        weave(w_woven[2], w_runs, 2 * CHUNK, 3 * CHUNK)
        for c in (1, 2):
            quantise_words(c)
        weave(w_woven[3], w_runs, 3 * CHUNK, V)
        quantise_words(3)

        results = [
            keep.tile([P, S], F32, name=f"result{c}", tag="w_places" if c == 2 else f"result{c}", align_bytes=64)
            for c in range(CHUNKS)
        ]

        def on_scalar(result, acc, c):
            nc.scalar.activation(result, acc, IDENTITY, bias=bias[c])

        def on_vector(result, acc, c):
            nc.vector.tensor_scalar(result, acc, bias[c], None, op0=ADD)

        last_quarter = S - QUARTER
        pieces = [(0, 0, QUARTER, on_scalar), (0, QUARTER, HALF, on_scalar), (0, HALF, S, on_scalar)]
        pieces = pieces + [(1, 0, HALF, on_scalar), (1, HALF, S, on_scalar)]
        pieces = pieces + [(2, 0, HALF, on_vector), (2, HALF, last_quarter, on_scalar), (2, last_quarter, S, on_vector)]
        pieces = pieces + [(3, 0, HALF, on_scalar), (3, HALF, last_quarter, on_vector), (3, last_quarter, S, on_scalar)]
        for n, (c, j0, j1, empty) in enumerate(pieces):
            rows = slice(CHUNK * c, CHUNK * (c + 1))
            acc = psum.tile([P, j1 - j0], F32, name=f"acc{n}", tag=f"bank{(n + 1) % BANKS}")
            nc.tensor.matmul_mx(
                out=acc[:],
                lhsT=w_codes[:, rows].bitcast(FP8X4),
                lhsT_scale=w_scales[:, rows],
                rhs=x_codes[:, j0:j1].bitcast(FP8X4),
                rhs_scale=x_scales[:, j0:j1],
                start=True,
                stop=True,
            )
            empty(results[c][:, j0:j1], acc[:], c)
            late_chunk = c >= 2
            if not late_chunk and j1 % HALF == 0:
                nc.sync.dma_start(out=out[rows, j1 - HALF : j1], in_=results[c][:, j1 - HALF : j1])
            if late_chunk and j1 == S:
                nc.sync.dma_start(out=out[rows, :], in_=results[c][:])
